import numpy as np
import ml_dtypes


def mxq(x, axis, fmt="e4m3"):
    dtype, down = {"e4m3": (ml_dtypes.float8_e4m3fn, 7), "e5m2": (ml_dtypes.float8_e5m2, 14)}[fmt]
    v = np.moveaxis(np.asarray(x, np.float32).astype(ml_dtypes.bfloat16).astype(np.float64), axis, -1)
    blocks = v.reshape(v.shape[:-1] + (-1, 32))
    amax = np.abs(blocks).max(-1, keepdims=True)
    byte = np.maximum(np.where(amax > 0, np.frexp(amax)[1] - 1 + 127, 0) - down, 1)
    scale = np.exp2(byte - 127.0)
    codes = (blocks / scale).astype(np.float32).astype(dtype).astype(np.float64)
    return np.moveaxis((codes * scale).reshape(v.shape), -1, axis)


WIDE = False


def mx_kscale(k):
    if not WIDE:
        return np.ones(k)
    levels = np.array([10, -10, 5, -5, 0])
    if k % 512:
        return np.exp2(np.random.permutation(np.resize(levels, k // 32))).repeat(32)
    a = np.empty((k // 512, 16))
    for p in range(k // 512):
        a[p, :8] = np.random.permutation(np.resize(levels, 8))
        for g in range(8):
            far = levels[np.abs(levels - a[p, g]) >= 10]
            a[p, g + 8] = far[np.random.randint(len(far))]
    return np.exp2(a.ravel()).repeat(32)


def f64(x):
    return np.asarray(x).astype(np.float64)


def striped(idx):
    return np.tile(idx.reshape(-1, 16).T, (8, 1)).astype(np.uint16)


def unstriped(offs):
    return offs[:16].T.reshape(-1).astype(np.int64)


def pack_weight(w):
    k, n = w.shape
    w = f64(np.asarray(w, np.float32).astype(ml_dtypes.bfloat16)).reshape(k // 32, 32, n)
    amax = np.abs(w).max(1)
    byte = np.clip(np.where(amax > 0, np.frexp(amax)[1] - 1 + 127 - 7, 1), 1, 254)
    scaled = (w * np.exp2(127.0 - byte)[:, None, :]).reshape(k, n).astype(np.float32)
    words = np.ascontiguousarray(scaled.reshape(k // 512, 128, 4, n).transpose(0, 1, 3, 2)).astype(ml_dtypes.float8_e4m3fn).view(np.uint8)
    return words, np.ascontiguousarray(byte.astype(np.uint8).reshape(k // 512, 16, n))


def unpack_weight(words, scales):
    g, p, n, _ = words.shape
    vals = np.ascontiguousarray(words).view(ml_dtypes.float8_e4m3fn).astype(np.float64) * np.repeat(np.exp2(scales.astype(np.float64) - 127.0), 8, axis=1)[..., None]
    return vals.transpose(0, 1, 3, 2).reshape(g * 512, n)


E2M1 = np.array([0.0, 0.5, 1.0, 1.5, 2.0, 3.0, 4.0, 6.0, -0.0, -0.5, -1.0, -1.5, -2.0, -3.0, -4.0, -6.0])


def pack_fp4(w):
    k, n = w.shape
    w = f64(np.asarray(w, np.float32).astype(ml_dtypes.bfloat16)).reshape(k // 32, 32, n)
    amax = np.abs(w).max(1)
    mant, ex = np.frexp(amax / 6.0)
    byte = np.clip(np.where(amax > 0, np.where(mant > 0.5, ex, ex - 1) + 127, 1), 1, 254)
    scaled = (w * np.exp2(127.0 - byte)[:, None, :]).reshape(k, n).astype(np.float32)
    c = np.ascontiguousarray(scaled.reshape(k // 512, 128, 4, n).transpose(0, 1, 3, 2)).astype(ml_dtypes.float4_e2m1fn).view(np.uint8) & 0xF
    words = (c[..., 0::2] | (c[..., 1::2] << 4)).reshape(k // 512, 128, 2 * n)
    return np.ascontiguousarray(words), np.ascontiguousarray(byte.astype(np.uint8).reshape(k // 512, 16, n))


def unpack_fp4(words, scales):
    g, _, n = scales.shape
    words = np.ascontiguousarray(words).reshape(g, 128, n, 2)
    nib = np.empty((g, 128, n, 4), np.uint8)
    nib[..., 0::2] = words & 0xF
    nib[..., 1::2] = words >> 4
    vals = E2M1[nib] * np.repeat(np.exp2(scales.astype(np.float64) - 127.0), 8, axis=1)[..., None]
    return vals.transpose(0, 1, 3, 2).reshape(g * 512, n)


def silu(v):
    return v / (1.0 + np.exp(-np.maximum(v, -700.0)))


K, T, S, H, N, U = 512, 4096, 1024, 512, 256, 2048
P = 2 ** 7


def setup_inputs():
    n = np.random.standard_normal
    s = mx_kscale(K)[:, None]
    u = mx_kscale(H)
    packed_xT = pack_weight(n((K, T)) * s)
    packed_w2 = pack_fp4(n((H, N)) / np.sqrt(H) / u[:, None])
    return {
        "x_words": packed_xT[0],
        "x_scales": packed_xT[1],
        "gate": np.tile(np.random.uniform(0.5, 1.5, S), (P, 1)).astype(np.float32),
        "w1": (n((K, H)) / np.sqrt(K) / s).astype(np.float32),
        "w3": (n((K, H)) / np.sqrt(K) / s * u).astype(np.float32),
        "w2_words": packed_w2[0],
        "w2_scales": packed_w2[1],
        "offs": striped(np.random.permutation(T)[:S]),
        "dst": striped(np.random.permutation(U)[:S]),
    }


def reference(x_words, x_scales, gate, w1, w3, w2_words, w2_scales, offs, dst):
    xq = unpack_weight(x_words, x_scales)[:, unstriped(offs)]
    h = (silu(mxq(f64(w1), 0, "e4m3").T @ xq)) * ((mxq(f64(w3), 0, "e4m3").T @ xq))
    y = unpack_fp4(w2_words, w2_scales).T @ mxq(h, 0, "e4m3")
    out = np.zeros((N, U))
    out[:, unstriped(dst)] = y * f64(gate)[:1]
    return out

@@ -1,0 +1,170 @@
+from contextlib import ExitStack
+
+import concourse.mybir as mybir
+
+K, T, S, H, N, U = 512, 4096, 1024, 512, 256, 2048
+FLOPS = 2 * S * K * H * 2 + 2 * S * H * N
+
+F32 = mybir.dt.float32
+BF16 = mybir.dt.bfloat16
+I32 = mybir.dt.int32
+U32 = mybir.dt.uint32
+U16 = mybir.dt.uint16
+U8 = mybir.dt.uint8
+FP8X4 = mybir.dt.float8_e4m3fn_x4
+FP4X4 = mybir.dt.float4_e2m1fn_x4
+MULT = mybir.AluOpType.mult
+SILU = mybir.ActivationFunctionType.Silu
+
+P = 128
+PACK = 4
+CHUNK = 128
+PAIR = 2 * CHUNK
+GATHER = 512
+AHEAD = 3
+W3_VECTOR = 80
+
+
+def tile_picked_route2_glusilu_p_kernel(tc, x_words, x_scales, gate, w1, w3, w2_words, w2_scales, offs, dst, out):
+    nc = tc.nc
+    with ExitStack() as ctx:
+        keep = ctx.enter_context(tc.tile_pool(name="keep", bufs=1))
+        psum_a = ctx.enter_context(tc.psum_pool(name="psum_a", bufs=3))
+        psum_b = ctx.enter_context(tc.psum_pool(name="psum_b", bufs=3))
+        psum_y = ctx.enter_context(tc.psum_pool(name="psum_y", bufs=2))
+
+        offs_sb = keep.tile([P, S // 16], U16, name="offs_sb")
+        dst_sb = keep.tile([P, S // 16], U16, name="dst_sb")
+        xs = keep.tile([P, T], U8, name="xs", align_bytes=64)
+        w1_raw = keep.tile([P, PACK, H], F32, name="w1_raw", tag="early", align_bytes=64)
+        w2w = keep.tile([P, 2 * N], U8, name="w2w", align_bytes=64)
+        w2s = keep.tile([P, N], U8, name="w2s", align_bytes=64)
+        warm_in = keep.tile([P, 1], F32, name="warm_in", tag="x_slot", align_bytes=64)
+        warm_out = keep.tile([P, 1], F32, name="warm_out", tag="w3_slot", align_bytes=64)
+        x_planes = keep.tile([P, S], U8, name="x_planes", align_bytes=64)
+
+        nc.vector.memset(xs[:].bitcast(I32), 0)
+        nc.vector.memset(warm_in[:], 0.0)
+        nc.vector.memset(w2s[:].bitcast(I32), 0)
+        nc.vector.memset(x_planes[:].bitcast(I32), 0)
+        nc.sync.dma_start(offs_sb[:], offs)
+        nc.sync.dma_start(w1_raw[:], w1.rearrange("(p j) c -> p j c", j=PACK))
+        nc.sync.dma_start(xs[0:P:8, :].bitcast(I32), x_scales[0].bitcast(I32))
+        nc.scalar.activation(warm_out[:], warm_in[:], SILU)
+        xw = keep.tile([P, T], U32, name="xw", tag="x_slot", align_bytes=64)
+        w3_raw = keep.tile([P, PACK, H], F32, name="w3_raw", tag="w3_slot", align_bytes=64)
+        nc.sync.dma_start(xw[:].bitcast(I32), x_words[0].rearrange("p n t -> p (n t)").bitcast(I32))
+        nc.sync.dma_start(w3_raw[:], w3.rearrange("(p j) c -> p j c", j=PACK))
+        nc.sync.dma_start(dst_sb[:], dst)
+        nc.gpsimd.dma_start(w2w[:].bitcast(I32), w2_words[0].bitcast(I32))
+        for q in range(4):
+            nc.gpsimd.dma_start(w2s[32 * q : 32 * q + 4, :].bitcast(I32), w2_scales[0, 4 * q : 4 * q + 4, :].bitcast(I32))
+
+        windows = [keep.tile([P, U], F32, name=f"window{m}") for m in range(N // P)]
+        for window in windows:
+            nc.vector.memset(window[:], 0.0)
+
+        def dealt(raw, grouped, m0, m1):
+            src = raw[:].rearrange("p j (m t) -> p m t j", t=PACK)[:, m0:m1]
+            to = grouped[:].rearrange("p (t m j) -> p m t j", t=PACK, j=PACK)[:, m0:m1]
+            return to, src
+
+        w1_bf = keep.tile([P, PACK * H], BF16, name="w1_bf", align_bytes=64)
+        w1_codes = keep.tile([P, H], U32, name="w1_codes", align_bytes=64)
+        w1_scales = keep.tile([P, H], U8, name="w1_scales", align_bytes=64)
+        w3_bf = keep.tile([P, PACK * H], BF16, name="w3_bf", align_bytes=64)
+        w3_codes = keep.tile([P, H], U32, name="w3_codes", align_bytes=64)
+        w3_scales = keep.tile([P, H], U8, name="w3_scales", align_bytes=64)
+
+        nc.scalar.copy(*dealt(w1_raw, w1_bf, 0, P))
+        gate_sb = keep.tile([P, PACK, H], F32, name="gate_sb", tag="early", align_bytes=64)
+        gate_row = gate_sb[:].rearrange("p j c -> p (j c)")
+        nc.sync.dma_start(gate_row[:, 0:S], gate)
+
+        picked_w = [keep.tile([P, GATHER], U32, name=f"picked_w{g}", align_bytes=64) for g in range(S // GATHER)]
+        picked_s = keep.tile([P, S], U8, name="picked_s", align_bytes=64)
+        nc.vector.tensor_copy(picked_s[:], xs[:].indirect(offs_sb[:]))
+        for r in range(4):
+            nc.scalar.dma_start(x_planes[r:P:32, :].bitcast(I32), picked_s[8 * r : P : 32, :].bitcast(I32))
+        nc.vector.quantize_mx(out=w1_codes[:].bitcast(FP8X4), scales=w1_scales[:], in_=w1_bf[:])
+        for g in range(S // GATHER):
+            cols = slice(g * GATHER // 16, (g + 1) * GATHER // 16)
+            nc.vector.tensor_copy(picked_w[g][:], xw[:].indirect(offs_sb[:, cols]))
+
+        def first_product(bank, codes, scales, c):
+            g, at = divmod(c * CHUNK, GATHER)
+            for t in range(PACK):
+                nc.tensor.matmul_mx(
+                    out=bank[:, t, :],
+                    lhsT=codes[:, t * P : (t + 1) * P].bitcast(FP8X4),
+                    lhsT_scale=scales[:, t * P : (t + 1) * P],
+                    rhs=picked_w[g][:, at : at + CHUNK].bitcast(FP8X4),
+                    rhs_scale=x_planes[:, c * CHUNK : (c + 1) * CHUNK],
+                    start=True,
+                    stop=True,
+                )
+
+        chunks = S // CHUNK
+        act = [keep.tile([P, CHUNK, PACK], F32, name=f"act{c}") for c in range(chunks)]
+        h_bf = [keep.tile([P, PAIR, PACK], BF16, name=f"h_bf{q}", align_bytes=64) for q in range(S // PAIR)]
+        h_codes = [keep.tile([P, PAIR], U32, name=f"h_codes{q}", align_bytes=64) for q in range(S // PAIR)]
+        h_scales = [keep.tile([P, PAIR], U8, name=f"h_scales{q}", align_bytes=64) for q in range(S // PAIR)]
+        y = [keep.tile([P, S], F32, name=f"y{m}") for m in range(N // P)]
+
+        def gate_branch(c):
+            bank = psum_a.tile([P, PACK, CHUNK], F32, name="bank_a")
+            first_product(bank, w1_codes, w1_scales, c)
+            nc.scalar.activation(act[c][:], bank[:].rearrange("p t n -> p n t"), SILU)
+
+        def hidden(c):
+            bank = psum_b.tile([P, PACK, CHUNK], F32, name="bank_b")
+            first_product(bank, w3_codes, w3_scales, c)
+            q, half = divmod(c, 2)
+            nc.vector.tensor_tensor(
+                h_bf[q][:, half * CHUNK : (half + 1) * CHUNK, :], bank[:].rearrange("p t n -> p n t"), act[c][:], MULT
+            )
+
+        def second_product(q):
+            nc.vector.quantize_mx(
+                out=h_codes[q][:].bitcast(FP8X4), scales=h_scales[q][:], in_=h_bf[q][:].rearrange("p n t -> p (n t)")
+            )
+            bank = psum_y.tile([P, N // P, PAIR], F32, name="bank_y")
+            for m in range(N // P):
+                nc.tensor.matmul_mx(
+                    out=bank[:, m, :],
+                    lhsT=w2w[:, 2 * m * P : 2 * (m + 1) * P].bitcast(FP4X4),
+                    lhsT_scale=w2s[:, m * P : (m + 1) * P],
+                    rhs=h_codes[q][:].bitcast(FP8X4),
+                    rhs_scale=h_scales[q][:],
+                    start=True,
+                    stop=True,
+                )
+            for m in range(N // P):
+                nc.scalar.copy(y[m][:, q * PAIR : (q + 1) * PAIR], bank[:, m, :])
+
+        def put(m, j0, j1):
+            nc.vector.tensor_tensor(
+                windows[m][:].indirect(dst_sb[:, j0 // 16 : j1 // 16]), y[m][:, j0:j1], gate_row[:, j0:j1], MULT
+            )
+
+        gate_branch(0)
+        nc.vector.tensor_copy(*dealt(w3_raw, w3_bf, 0, W3_VECTOR))
+        nc.scalar.copy(*dealt(w3_raw, w3_bf, W3_VECTOR, P))
+        nc.vector.quantize_mx(out=w3_codes[:].bitcast(FP8X4), scales=w3_scales[:], in_=w3_bf[:])
+        for c in range(1, AHEAD):
+            gate_branch(c)
+        for c in range(chunks):
+            hidden(c)
+            if c + AHEAD < chunks:
+                gate_branch(c + AHEAD)
+            if c >= 2 and c % 2 == 0:
+                second_product(c // 2 - 1)
+        last = S // PAIR - 1
+        put(0, 0, PAIR)
+        second_product(last)
+        put(0, PAIR, last * PAIR)
+        put(0, last * PAIR, S)
+        nc.sync.dma_start(out[0:P, :], windows[0][:])
+        put(1, 0, S)
+        nc.sync.dma_start(out[P : 2 * P, 0 : U // 2], windows[1][:, 0 : U // 2])
+        nc.scalar.dma_start(out[P : 2 * P, U // 2 : U], windows[1][:, U // 2 : U])

@@ -21,72 +21,67 @@ PACK = 4
 CHUNK = 128
 PAIR = 2 * CHUNK
 GATHER = 512
-AHEAD = 3
-W3_VECTOR = 80
+AHEAD = 4
 
 
 def tile_picked_route2_glusilu_p_kernel(tc, x_words, x_scales, gate, w1, w3, w2_words, w2_scales, offs, dst, out):
     nc = tc.nc
     with ExitStack() as ctx:
         keep = ctx.enter_context(tc.tile_pool(name="keep", bufs=1))
-        psum_a = ctx.enter_context(tc.psum_pool(name="psum_a", bufs=3))
+        psum_a = ctx.enter_context(tc.psum_pool(name="psum_a", bufs=4))
         psum_b = ctx.enter_context(tc.psum_pool(name="psum_b", bufs=3))
-        psum_y = ctx.enter_context(tc.psum_pool(name="psum_y", bufs=2))
+        psum_y = ctx.enter_context(tc.psum_pool(name="psum_y", bufs=1))
 
         offs_sb = keep.tile([P, S // 16], U16, name="offs_sb")
         dst_sb = keep.tile([P, S // 16], U16, name="dst_sb")
-        xs = keep.tile([P, T], U8, name="xs", align_bytes=64)
+        xs = keep.tile([P, T], U8, name="xs", tag="xs_slot", align_bytes=64)
         w1_raw = keep.tile([P, PACK, H], F32, name="w1_raw", tag="early", align_bytes=64)
         w2w = keep.tile([P, 2 * N], U8, name="w2w", align_bytes=64)
-        w2s = keep.tile([P, N], U8, name="w2s", align_bytes=64)
         warm_in = keep.tile([P, 1], F32, name="warm_in", tag="x_slot", align_bytes=64)
         warm_out = keep.tile([P, 1], F32, name="warm_out", tag="w3_slot", align_bytes=64)
-        x_planes = keep.tile([P, S], U8, name="x_planes", align_bytes=64)
 
-        nc.vector.memset(xs[:].bitcast(I32), 0)
         nc.vector.memset(warm_in[:], 0.0)
-        nc.vector.memset(w2s[:].bitcast(I32), 0)
-        nc.vector.memset(x_planes[:].bitcast(I32), 0)
+        nc.gpsimd.memset(xs[:].bitcast(I32), 0)
         nc.sync.dma_start(offs_sb[:], offs)
         nc.sync.dma_start(w1_raw[:], w1.rearrange("(p j) c -> p j c", j=PACK))
-        nc.sync.dma_start(xs[0:P:8, :].bitcast(I32), x_scales[0].bitcast(I32))
+        nc.sync.dma_start(dst_sb[:], dst)
+        nc.sync.dma_start(w2w[:].bitcast(I32), w2_words[0].bitcast(I32))
+        for r in range(4):
+            nc.sync.dma_start(xs[r:P:32, :].bitcast(I32), x_scales[0, r:16:4, :].bitcast(I32))
         nc.scalar.activation(warm_out[:], warm_in[:], SILU)
         xw = keep.tile([P, T], U32, name="xw", tag="x_slot", align_bytes=64)
-        w3_raw = keep.tile([P, PACK, H], F32, name="w3_raw", tag="w3_slot", align_bytes=64)
         nc.sync.dma_start(xw[:].bitcast(I32), x_words[0].rearrange("p n t -> p (n t)").bitcast(I32))
+        w3_raw = keep.tile([P, PACK, H], F32, name="w3_raw", tag="w3_slot", align_bytes=64)
         nc.sync.dma_start(w3_raw[:], w3.rearrange("(p j) c -> p j c", j=PACK))
-        nc.sync.dma_start(dst_sb[:], dst)
-        nc.gpsimd.dma_start(w2w[:].bitcast(I32), w2_words[0].bitcast(I32))
-        for q in range(4):
-            nc.gpsimd.dma_start(w2s[32 * q : 32 * q + 4, :].bitcast(I32), w2_scales[0, 4 * q : 4 * q + 4, :].bitcast(I32))
 
         windows = [keep.tile([P, U], F32, name=f"window{m}") for m in range(N // P)]
         for window in windows:
-            nc.vector.memset(window[:], 0.0)
+            nc.gpsimd.memset(window[:], 0.0)
 
-        def dealt(raw, grouped, m0, m1):
-            src = raw[:].rearrange("p j (m t) -> p m t j", t=PACK)[:, m0:m1]
-            to = grouped[:].rearrange("p (t m j) -> p m t j", t=PACK, j=PACK)[:, m0:m1]
+        def dealt(raw, grouped, t0, t1):
+            src = raw[:].rearrange("p j (m t) -> p m t j", t=PACK)[:, :, t0:t1, :]
+            to = grouped[:].rearrange("p (t m j) -> p m t j", m=P, j=PACK)
             return to, src
 
-        w1_bf = keep.tile([P, PACK * H], BF16, name="w1_bf", align_bytes=64)
+        w1_bf = keep.tile([P, PACK * H], BF16, name="w1_bf", tag="w1_bf", align_bytes=64)
         w1_codes = keep.tile([P, H], U32, name="w1_codes", align_bytes=64)
-        w1_scales = keep.tile([P, H], U8, name="w1_scales", align_bytes=64)
-        w3_bf = keep.tile([P, PACK * H], BF16, name="w3_bf", align_bytes=64)
+        w3_bf = [keep.tile([P, PACK * H // 2], BF16, name=f"w3_bf{u}", align_bytes=64) for u in range(2)]
         w3_codes = keep.tile([P, H], U32, name="w3_codes", align_bytes=64)
         w3_scales = keep.tile([P, H], U8, name="w3_scales", align_bytes=64)
 
-        nc.scalar.copy(*dealt(w1_raw, w1_bf, 0, P))
-        gate_sb = keep.tile([P, PACK, H], F32, name="gate_sb", tag="early", align_bytes=64)
-        gate_row = gate_sb[:].rearrange("p j c -> p (j c)")
-        nc.sync.dma_start(gate_row[:, 0:S], gate)
+        nc.scalar.copy(*dealt(w1_raw, w1_bf, 0, PACK))
 
         picked_w = [keep.tile([P, GATHER], U32, name=f"picked_w{g}", align_bytes=64) for g in range(S // GATHER)]
         picked_s = keep.tile([P, S], U8, name="picked_s", align_bytes=64)
         nc.vector.tensor_copy(picked_s[:], xs[:].indirect(offs_sb[:]))
-        for r in range(4):
-            nc.scalar.dma_start(x_planes[r:P:32, :].bitcast(I32), picked_s[8 * r : P : 32, :].bitcast(I32))
+        gate_row = keep.tile([P, S], F32, name="gate_row", tag="early", align_bytes=64)
+        nc.sync.dma_start(gate_row[:], gate)
+        w1_scales = keep.tile([P, H], U8, name="w1_scales", tag="xs_slot", align_bytes=64)
         nc.vector.quantize_mx(out=w1_codes[:].bitcast(FP8X4), scales=w1_scales[:], in_=w1_bf[:])
+        w2s = keep.tile([P, N], U8, name="w2s", tag="w1_bf", align_bytes=64)
+        nc.vector.memset(w2s[:].bitcast(I32), 0)
+        for r in range(4):
+            nc.sync.dma_start(w2s[r:P:32, :].bitcast(I32), w2_scales[0, r:16:4, :].bitcast(I32))
         for g in range(S // GATHER):
             cols = slice(g * GATHER // 16, (g + 1) * GATHER // 16)
             nc.vector.tensor_copy(picked_w[g][:], xw[:].indirect(offs_sb[:, cols]))
@@ -99,13 +94,13 @@ def tile_picked_route2_glusilu_p_kernel(tc, x_words, x_scales, gate, w1, w3, w2_
                     lhsT=codes[:, t * P : (t + 1) * P].bitcast(FP8X4),
                     lhsT_scale=scales[:, t * P : (t + 1) * P],
                     rhs=picked_w[g][:, at : at + CHUNK].bitcast(FP8X4),
-                    rhs_scale=x_planes[:, c * CHUNK : (c + 1) * CHUNK],
+                    rhs_scale=picked_s[:, c * CHUNK : (c + 1) * CHUNK],
                     start=True,
                     stop=True,
                 )
 
         chunks = S // CHUNK
-        act = [keep.tile([P, CHUNK, PACK], F32, name=f"act{c}") for c in range(chunks)]
+        act = []
         h_bf = [keep.tile([P, PAIR, PACK], BF16, name=f"h_bf{q}", align_bytes=64) for q in range(S // PAIR)]
         h_codes = [keep.tile([P, PAIR], U32, name=f"h_codes{q}", align_bytes=64) for q in range(S // PAIR)]
         h_scales = [keep.tile([P, PAIR], U8, name=f"h_scales{q}", align_bytes=64) for q in range(S // PAIR)]
@@ -114,6 +109,8 @@ def tile_picked_route2_glusilu_p_kernel(tc, x_words, x_scales, gate, w1, w3, w2_
         def gate_branch(c):
             bank = psum_a.tile([P, PACK, CHUNK], F32, name="bank_a")
             first_product(bank, w1_codes, w1_scales, c)
+            tag = "w3_slot" if c == 1 else f"act{c}"
+            act.append(keep.tile([P, CHUNK, PACK], F32, name=f"act{c}", tag=tag, align_bytes=64))
             nc.scalar.activation(act[c][:], bank[:].rearrange("p t n -> p n t"), SILU)
 
         def hidden(c):
@@ -148,9 +145,11 @@ def tile_picked_route2_glusilu_p_kernel(tc, x_words, x_scales, gate, w1, w3, w2_
             )
 
         gate_branch(0)
-        nc.vector.tensor_copy(*dealt(w3_raw, w3_bf, 0, W3_VECTOR))
-        nc.scalar.copy(*dealt(w3_raw, w3_bf, W3_VECTOR, P))
-        nc.vector.quantize_mx(out=w3_codes[:].bitcast(FP8X4), scales=w3_scales[:], in_=w3_bf[:])
+        nc.vector.tensor_copy(*dealt(w3_raw, w3_bf[0], 0, 2))
+        nc.scalar.copy(*dealt(w3_raw, w3_bf[1], 2, PACK))
+        for u in range(2):
+            cols = slice(u * H // 2, (u + 1) * H // 2)
+            nc.vector.quantize_mx(out=w3_codes[:, cols].bitcast(FP8X4), scales=w3_scales[:, cols], in_=w3_bf[u][:])
         for c in range(1, AHEAD):
             gate_branch(c)
         for c in range(chunks):

@@ -28,6 +28,7 @@ def tile_picked_route2_glusilu_p_kernel(tc, x_words, x_scales, gate, w1, w3, w2_
     nc = tc.nc
     with ExitStack() as ctx:
         keep = ctx.enter_context(tc.tile_pool(name="keep", bufs=1))
+        reuse = ctx.enter_context(tc.tile_pool(name="reuse", bufs=1))
         psum_a = ctx.enter_context(tc.psum_pool(name="psum_a", bufs=4))
         psum_b = ctx.enter_context(tc.psum_pool(name="psum_b", bufs=3))
         psum_y = ctx.enter_context(tc.psum_pool(name="psum_y", bufs=1))
@@ -36,27 +37,26 @@ def tile_picked_route2_glusilu_p_kernel(tc, x_words, x_scales, gate, w1, w3, w2_
         dst_sb = keep.tile([P, S // 16], U16, name="dst_sb")
         xs = keep.tile([P, T], U8, name="xs", tag="xs_slot", align_bytes=64)
         w1_raw = keep.tile([P, PACK, H], F32, name="w1_raw", tag="early", align_bytes=64)
-        w2w = keep.tile([P, 2 * N], U8, name="w2w", align_bytes=64)
-        warm_in = keep.tile([P, 1], F32, name="warm_in", tag="x_slot", align_bytes=64)
-        warm_out = keep.tile([P, 1], F32, name="warm_out", tag="w3_slot", align_bytes=64)
+        warm_in = reuse.tile([P, 32], F32, name="warm_in", offset=4 * T - 64, align_bytes=64)
+        warm_out = keep.tile([P, 32], F32, name="warm_out")
+        x_planes = keep.tile([P, S], U8, name="x_planes", align_bytes=64)
 
         nc.vector.memset(warm_in[:], 0.0)
         nc.gpsimd.memset(xs[:].bitcast(I32), 0)
+        nc.vector.memset(x_planes[:].bitcast(I32), 0)
         nc.sync.dma_start(offs_sb[:], offs)
         nc.sync.dma_start(w1_raw[:], w1.rearrange("(p j) c -> p j c", j=PACK))
         nc.sync.dma_start(dst_sb[:], dst)
-        nc.sync.dma_start(w2w[:].bitcast(I32), w2_words[0].bitcast(I32))
-        for r in range(4):
-            nc.sync.dma_start(xs[r:P:32, :].bitcast(I32), x_scales[0, r:16:4, :].bitcast(I32))
+        nc.sync.dma_start(xs[0:P:8, :].bitcast(I32), x_scales[0].bitcast(I32))
         nc.scalar.activation(warm_out[:], warm_in[:], SILU)
-        xw = keep.tile([P, T], U32, name="xw", tag="x_slot", align_bytes=64)
+        xw = reuse.tile([P, T], U32, name="xw", offset=0, align_bytes=64)
         nc.sync.dma_start(xw[:].bitcast(I32), x_words[0].rearrange("p n t -> p (n t)").bitcast(I32))
-        w3_raw = keep.tile([P, PACK, H], F32, name="w3_raw", tag="w3_slot", align_bytes=64)
+        w3_raw = reuse.tile([P, PACK, H], F32, name="w3_raw", offset=4 * T, align_bytes=64)
         nc.sync.dma_start(w3_raw[:], w3.rearrange("(p j) c -> p j c", j=PACK))
 
         windows = [keep.tile([P, U], F32, name=f"window{m}") for m in range(N // P)]
         for window in windows:
-            nc.gpsimd.memset(window[:], 0.0)
+            nc.vector.memset(window[:], 0.0)
 
         def dealt(raw, grouped, t0, t1):
             src = raw[:].rearrange("p j (m t) -> p m t j", t=PACK)[:, :, t0:t1, :]
@@ -74,8 +74,10 @@ def tile_picked_route2_glusilu_p_kernel(tc, x_words, x_scales, gate, w1, w3, w2_
         picked_w = [keep.tile([P, GATHER], U32, name=f"picked_w{g}", align_bytes=64) for g in range(S // GATHER)]
         picked_s = keep.tile([P, S], U8, name="picked_s", align_bytes=64)
         nc.vector.tensor_copy(picked_s[:], xs[:].indirect(offs_sb[:]))
-        gate_row = keep.tile([P, S], F32, name="gate_row", tag="early", align_bytes=64)
-        nc.sync.dma_start(gate_row[:], gate)
+        for r in range(4):
+            nc.scalar.dma_start(x_planes[r:P:32, :].bitcast(I32), picked_s[8 * r : P : 32, :].bitcast(I32))
+        w2w = keep.tile([P, 2 * N], U8, name="w2w", tag="early", align_bytes=64)
+        nc.sync.dma_start(w2w[:].bitcast(I32), w2_words[0].bitcast(I32))
         w1_scales = keep.tile([P, H], U8, name="w1_scales", tag="xs_slot", align_bytes=64)
         nc.vector.quantize_mx(out=w1_codes[:].bitcast(FP8X4), scales=w1_scales[:], in_=w1_bf[:])
         w2s = keep.tile([P, N], U8, name="w2s", tag="w1_bf", align_bytes=64)
@@ -85,6 +87,8 @@ def tile_picked_route2_glusilu_p_kernel(tc, x_words, x_scales, gate, w1, w3, w2_
         for g in range(S // GATHER):
             cols = slice(g * GATHER // 16, (g + 1) * GATHER // 16)
             nc.vector.tensor_copy(picked_w[g][:], xw[:].indirect(offs_sb[:, cols]))
+        gate_row = reuse.tile([P, S], F32, name="gate_row", offset=0, align_bytes=64)
+        nc.sync.dma_start(gate_row[:], gate)
 
         def first_product(bank, codes, scales, c):
             g, at = divmod(c * CHUNK, GATHER)
@@ -94,23 +98,21 @@ def tile_picked_route2_glusilu_p_kernel(tc, x_words, x_scales, gate, w1, w3, w2_
                     lhsT=codes[:, t * P : (t + 1) * P].bitcast(FP8X4),
                     lhsT_scale=scales[:, t * P : (t + 1) * P],
                     rhs=picked_w[g][:, at : at + CHUNK].bitcast(FP8X4),
-                    rhs_scale=picked_s[:, c * CHUNK : (c + 1) * CHUNK],
+                    rhs_scale=x_planes[:, c * CHUNK : (c + 1) * CHUNK],
                     start=True,
                     stop=True,
                 )
 
         chunks = S // CHUNK
-        act = []
+        act = [keep.tile([P, CHUNK, PACK], F32, name=f"act{c}") for c in range(chunks)]
         h_bf = [keep.tile([P, PAIR, PACK], BF16, name=f"h_bf{q}", align_bytes=64) for q in range(S // PAIR)]
         h_codes = [keep.tile([P, PAIR], U32, name=f"h_codes{q}", align_bytes=64) for q in range(S // PAIR)]
         h_scales = [keep.tile([P, PAIR], U8, name=f"h_scales{q}", align_bytes=64) for q in range(S // PAIR)]
-        y = [keep.tile([P, S], F32, name=f"y{m}") for m in range(N // P)]
+        y = keep.tile([P, N // P, S], F32, name="y")
 
         def gate_branch(c):
             bank = psum_a.tile([P, PACK, CHUNK], F32, name="bank_a")
             first_product(bank, w1_codes, w1_scales, c)
-            tag = "w3_slot" if c == 1 else f"act{c}"
-            act.append(keep.tile([P, CHUNK, PACK], F32, name=f"act{c}", tag=tag, align_bytes=64))
             nc.scalar.activation(act[c][:], bank[:].rearrange("p t n -> p n t"), SILU)
 
         def hidden(c):
@@ -136,21 +138,19 @@ def tile_picked_route2_glusilu_p_kernel(tc, x_words, x_scales, gate, w1, w3, w2_
                     start=True,
                     stop=True,
                 )
-            for m in range(N // P):
-                nc.scalar.copy(y[m][:, q * PAIR : (q + 1) * PAIR], bank[:, m, :])
+            nc.scalar.copy(y[:, :, q * PAIR : (q + 1) * PAIR], bank[:])
 
         def put(m, j0, j1):
             nc.vector.tensor_tensor(
-                windows[m][:].indirect(dst_sb[:, j0 // 16 : j1 // 16]), y[m][:, j0:j1], gate_row[:, j0:j1], MULT
+                windows[m][:].indirect(dst_sb[:, j0 // 16 : j1 // 16]), y[:, m, j0:j1], gate_row[:, j0:j1], MULT
             )
 
-        gate_branch(0)
-        nc.vector.tensor_copy(*dealt(w3_raw, w3_bf[0], 0, 2))
-        nc.scalar.copy(*dealt(w3_raw, w3_bf[1], 2, PACK))
+        for u in range(2):
+            nc.vector.tensor_copy(*dealt(w3_raw, w3_bf[u], 2 * u, 2 * u + 2))
         for u in range(2):
             cols = slice(u * H // 2, (u + 1) * H // 2)
             nc.vector.quantize_mx(out=w3_codes[:, cols].bitcast(FP8X4), scales=w3_scales[:, cols], in_=w3_bf[u][:])
-        for c in range(1, AHEAD):
+        for c in range(AHEAD):
             gate_branch(c)
         for c in range(chunks):
             hidden(c)

@@ -21,7 +21,8 @@ PACK = 4
 CHUNK = 128
 PAIR = 2 * CHUNK
 GATHER = 512
-AHEAD = 4
+AHEAD = 5
+SHARED = 2
 
 
 def tile_picked_route2_glusilu_p_kernel(tc, x_words, x_scales, gate, w1, w3, w2_words, w2_scales, offs, dst, out):
@@ -29,9 +30,8 @@ def tile_picked_route2_glusilu_p_kernel(tc, x_words, x_scales, gate, w1, w3, w2_
     with ExitStack() as ctx:
         keep = ctx.enter_context(tc.tile_pool(name="keep", bufs=1))
         reuse = ctx.enter_context(tc.tile_pool(name="reuse", bufs=1))
-        psum_a = ctx.enter_context(tc.psum_pool(name="psum_a", bufs=4))
+        psum_a = ctx.enter_context(tc.psum_pool(name="psum_a", bufs=5))
         psum_b = ctx.enter_context(tc.psum_pool(name="psum_b", bufs=3))
-        psum_y = ctx.enter_context(tc.psum_pool(name="psum_y", bufs=1))
 
         offs_sb = keep.tile([P, S // 16], U16, name="offs_sb")
         dst_sb = keep.tile([P, S // 16], U16, name="dst_sb")
@@ -105,44 +105,51 @@ def tile_picked_route2_glusilu_p_kernel(tc, x_words, x_scales, gate, w1, w3, w2_
 
         chunks = S // CHUNK
         act = [keep.tile([P, CHUNK, PACK], F32, name=f"act{c}") for c in range(chunks)]
-        h_bf = [keep.tile([P, PAIR, PACK], BF16, name=f"h_bf{q}", align_bytes=64) for q in range(S // PAIR)]
-        h_codes = [keep.tile([P, PAIR], U32, name=f"h_codes{q}", align_bytes=64) for q in range(S // PAIR)]
-        h_scales = [keep.tile([P, PAIR], U8, name=f"h_scales{q}", align_bytes=64) for q in range(S // PAIR)]
-        y = keep.tile([P, N // P, S], F32, name="y")
+        h_bf = keep.tile([P, S * PACK], BF16, name="h_bf", align_bytes=64)
+        h_codes = keep.tile([P, S], U32, name="h_codes", align_bytes=64)
+        h_scales = keep.tile([P, S], U8, name="h_scales", align_bytes=64)
+        y = [keep.tile([P, S], F32, name=f"y{m}") for m in range(N // P)]
+
+        def h_of(c):
+            return h_bf[:, c * CHUNK * PACK : (c + 1) * CHUNK * PACK].rearrange("p (n t) -> p n t", t=PACK)
 
         def gate_branch(c):
-            bank = psum_a.tile([P, PACK, CHUNK], F32, name="bank_a")
+            bank = psum_a.tile([P, PACK, CHUNK], F32, name="bank_a", tag="ring")
             first_product(bank, w1_codes, w1_scales, c)
             nc.scalar.activation(act[c][:], bank[:].rearrange("p t n -> p n t"), SILU)
 
         def hidden(c):
             bank = psum_b.tile([P, PACK, CHUNK], F32, name="bank_b")
             first_product(bank, w3_codes, w3_scales, c)
-            q, half = divmod(c, 2)
-            nc.vector.tensor_tensor(
-                h_bf[q][:, half * CHUNK : (half + 1) * CHUNK, :], bank[:].rearrange("p t n -> p n t"), act[c][:], MULT
-            )
+            nc.vector.tensor_tensor(h_of(c), bank[:].rearrange("p t n -> p n t"), act[c][:], MULT)
 
-        def second_product(q):
+        def hidden_aside(c):
+            bank = psum_a.tile([P, PACK, CHUNK], F32, name="bank_c", tag="ring")
+            first_product(bank, w3_codes, w3_scales, c)
+            lin = keep.tile([P, CHUNK, PACK], F32, name=f"lin{c}")
+            nc.scalar.copy(lin[:], bank[:].rearrange("p t n -> p n t"))
+            nc.gpsimd.tensor_tensor(h_of(c), lin[:], act[c][:], MULT)
+
+        def second_product(j0, j1):
             nc.vector.quantize_mx(
-                out=h_codes[q][:].bitcast(FP8X4), scales=h_scales[q][:], in_=h_bf[q][:].rearrange("p n t -> p (n t)")
+                out=h_codes[:, j0:j1].bitcast(FP8X4), scales=h_scales[:, j0:j1], in_=h_bf[:, PACK * j0 : PACK * j1]
             )
-            bank = psum_y.tile([P, N // P, PAIR], F32, name="bank_y")
             for m in range(N // P):
+                bank = psum_a.tile([P, j1 - j0], F32, name="bank_y", tag="ring")
                 nc.tensor.matmul_mx(
-                    out=bank[:, m, :],
+                    out=bank[:],
                     lhsT=w2w[:, 2 * m * P : 2 * (m + 1) * P].bitcast(FP4X4),
                     lhsT_scale=w2s[:, m * P : (m + 1) * P],
-                    rhs=h_codes[q][:].bitcast(FP8X4),
-                    rhs_scale=h_scales[q][:],
+                    rhs=h_codes[:, j0:j1].bitcast(FP8X4),
+                    rhs_scale=h_scales[:, j0:j1],
                     start=True,
                     stop=True,
                 )
-            nc.scalar.copy(y[:, :, q * PAIR : (q + 1) * PAIR], bank[:])
+                nc.scalar.copy(y[m][:, j0:j1], bank[:])
 
         def put(m, j0, j1):
             nc.vector.tensor_tensor(
-                windows[m][:].indirect(dst_sb[:, j0 // 16 : j1 // 16]), y[:, m, j0:j1], gate_row[:, j0:j1], MULT
+                windows[m][:].indirect(dst_sb[:, j0 // 16 : j1 // 16]), y[m][:, j0:j1], gate_row[:, j0:j1], MULT
             )
 
         for u in range(2):
@@ -152,17 +159,19 @@ def tile_picked_route2_glusilu_p_kernel(tc, x_words, x_scales, gate, w1, w3, w2_
             nc.vector.quantize_mx(out=w3_codes[:, cols].bitcast(FP8X4), scales=w3_scales[:, cols], in_=w3_bf[u][:])
         for c in range(AHEAD):
             gate_branch(c)
-        for c in range(chunks):
+        for c in range(chunks - SHARED):
             hidden(c)
             if c + AHEAD < chunks:
                 gate_branch(c + AHEAD)
+            if c + AHEAD == chunks - 1:
+                for aside in range(chunks - SHARED, chunks):
+                    hidden_aside(aside)
             if c >= 2 and c % 2 == 0:
-                second_product(c // 2 - 1)
-        last = S // PAIR - 1
+                second_product((c - 2) * CHUNK, c * CHUNK)
         put(0, 0, PAIR)
-        second_product(last)
-        put(0, PAIR, last * PAIR)
-        put(0, last * PAIR, S)
+        second_product(S // 2, S)
+        put(0, PAIR, S // 2)
+        put(0, S // 2, S)
         nc.sync.dma_start(out[0:P, :], windows[0][:])
         put(1, 0, S)
         nc.sync.dma_start(out[P : 2 * P, 0 : U // 2], windows[1][:, 0 : U // 2])

@@ -21,8 +21,7 @@ PACK = 4
 CHUNK = 128
 PAIR = 2 * CHUNK
 GATHER = 512
-AHEAD = 5
-SHARED = 2
+ASIDE = (2, 3)
 
 
 def tile_picked_route2_glusilu_p_kernel(tc, x_words, x_scales, gate, w1, w3, w2_words, w2_scales, offs, dst, out):
@@ -30,33 +29,27 @@ def tile_picked_route2_glusilu_p_kernel(tc, x_words, x_scales, gate, w1, w3, w2_
     with ExitStack() as ctx:
         keep = ctx.enter_context(tc.tile_pool(name="keep", bufs=1))
         reuse = ctx.enter_context(tc.tile_pool(name="reuse", bufs=1))
-        psum_a = ctx.enter_context(tc.psum_pool(name="psum_a", bufs=5))
-        psum_b = ctx.enter_context(tc.psum_pool(name="psum_b", bufs=3))
+        psum_a = ctx.enter_context(tc.psum_pool(name="psum_a", bufs=4))
+        psum_b = ctx.enter_context(tc.psum_pool(name="psum_b", bufs=4))
 
         offs_sb = keep.tile([P, S // 16], U16, name="offs_sb")
         dst_sb = keep.tile([P, S // 16], U16, name="dst_sb")
-        xs = keep.tile([P, T], U8, name="xs", tag="xs_slot", align_bytes=64)
+        xs = reuse.tile([P, T], U8, name="xs", offset=3 * T // 2, align_bytes=64)
         w1_raw = keep.tile([P, PACK, H], F32, name="w1_raw", tag="early", align_bytes=64)
-        warm_in = reuse.tile([P, 32], F32, name="warm_in", offset=4 * T - 64, align_bytes=64)
-        warm_out = keep.tile([P, 32], F32, name="warm_out")
+        xw = keep.tile([P, T], U32, name="xw", tag="xw_slot", align_bytes=64)
+        zeros = keep.tile([P, 32], F32, name="zeros")
         x_planes = keep.tile([P, S], U8, name="x_planes", align_bytes=64)
+        window1 = keep.tile([P, U], F32, name="window1")
 
-        nc.vector.memset(warm_in[:], 0.0)
-        nc.gpsimd.memset(xs[:].bitcast(I32), 0)
-        nc.vector.memset(x_planes[:].bitcast(I32), 0)
+        nc.sync.dma_start(xs[112:P, :].bitcast(I32), x_scales[0].bitcast(I32))
         nc.sync.dma_start(offs_sb[:], offs)
         nc.sync.dma_start(w1_raw[:], w1.rearrange("(p j) c -> p j c", j=PACK))
-        nc.sync.dma_start(dst_sb[:], dst)
-        nc.sync.dma_start(xs[0:P:8, :].bitcast(I32), x_scales[0].bitcast(I32))
-        nc.scalar.activation(warm_out[:], warm_in[:], SILU)
-        xw = reuse.tile([P, T], U32, name="xw", offset=0, align_bytes=64)
         nc.sync.dma_start(xw[:].bitcast(I32), x_words[0].rearrange("p n t -> p (n t)").bitcast(I32))
-        w3_raw = reuse.tile([P, PACK, H], F32, name="w3_raw", offset=4 * T, align_bytes=64)
-        nc.sync.dma_start(w3_raw[:], w3.rearrange("(p j) c -> p j c", j=PACK))
-
-        windows = [keep.tile([P, U], F32, name=f"window{m}") for m in range(N // P)]
-        for window in windows:
-            nc.vector.memset(window[:], 0.0)
+        nc.sync.dma_start(dst_sb[:], dst)
+        nc.vector.memset(zeros[:], 0.0)
+        nc.scalar.activation(window1[:], zeros[:, 0:1].to_broadcast([P, U]), SILU)
+        nc.vector.memset(xs[0:112, :].bitcast(I32), 0)
+        nc.vector.memset(x_planes[:].bitcast(I32), 0)
 
         def dealt(raw, grouped, t0, t1):
             src = raw[:].rearrange("p j (m t) -> p m t j", t=PACK)[:, :, t0:t1, :]
@@ -65,7 +58,7 @@ def tile_picked_route2_glusilu_p_kernel(tc, x_words, x_scales, gate, w1, w3, w2_
 
         w1_bf = keep.tile([P, PACK * H], BF16, name="w1_bf", tag="w1_bf", align_bytes=64)
         w1_codes = keep.tile([P, H], U32, name="w1_codes", align_bytes=64)
-        w3_bf = [keep.tile([P, PACK * H // 2], BF16, name=f"w3_bf{u}", align_bytes=64) for u in range(2)]
+        w3_bf = [keep.tile([P, PACK * H // 2], BF16, name=f"w3_bf{u}", tag=f"w3_bf{u}", align_bytes=64) for u in range(2)]
         w3_codes = keep.tile([P, H], U32, name="w3_codes", align_bytes=64)
         w3_scales = keep.tile([P, H], U8, name="w3_scales", align_bytes=64)
 
@@ -75,10 +68,17 @@ def tile_picked_route2_glusilu_p_kernel(tc, x_words, x_scales, gate, w1, w3, w2_
         picked_s = keep.tile([P, S], U8, name="picked_s", align_bytes=64)
         nc.vector.tensor_copy(picked_s[:], xs[:].indirect(offs_sb[:]))
         for r in range(4):
-            nc.scalar.dma_start(x_planes[r:P:32, :].bitcast(I32), picked_s[8 * r : P : 32, :].bitcast(I32))
+            nc.sync.dma_start(
+                x_planes[32 * r : 32 * r + 4, :].bitcast(I32), picked_s[112 + 4 * r : 116 + 4 * r, :].bitcast(I32)
+            )
+        w3_raw = reuse.tile([P, PACK, H], F32, name="w3_raw", offset=0, align_bytes=64)
+        nc.sync.dma_start(w3_raw[:], w3.rearrange("(p j) c -> p j c", j=PACK))
+        window0 = reuse.tile([P, U], F32, name="window0", offset=2 * T, align_bytes=64)
+        nc.vector.memset(window0[:], 0.0)
+        windows = [window0, window1]
         w2w = keep.tile([P, 2 * N], U8, name="w2w", tag="early", align_bytes=64)
         nc.sync.dma_start(w2w[:].bitcast(I32), w2_words[0].bitcast(I32))
-        w1_scales = keep.tile([P, H], U8, name="w1_scales", tag="xs_slot", align_bytes=64)
+        w1_scales = keep.tile([P, H], U8, name="w1_scales", align_bytes=64)
         nc.vector.quantize_mx(out=w1_codes[:].bitcast(FP8X4), scales=w1_scales[:], in_=w1_bf[:])
         w2s = keep.tile([P, N], U8, name="w2s", tag="w1_bf", align_bytes=64)
         nc.vector.memset(w2s[:].bitcast(I32), 0)
@@ -87,7 +87,7 @@ def tile_picked_route2_glusilu_p_kernel(tc, x_words, x_scales, gate, w1, w3, w2_
         for g in range(S // GATHER):
             cols = slice(g * GATHER // 16, (g + 1) * GATHER // 16)
             nc.vector.tensor_copy(picked_w[g][:], xw[:].indirect(offs_sb[:, cols]))
-        gate_row = reuse.tile([P, S], F32, name="gate_row", offset=0, align_bytes=64)
+        gate_row = keep.tile([P, S], F32, name="gate_row", tag="xw_slot", align_bytes=64)
         nc.sync.dma_start(gate_row[:], gate)
 
         def first_product(bank, codes, scales, c):
@@ -104,11 +104,11 @@ def tile_picked_route2_glusilu_p_kernel(tc, x_words, x_scales, gate, w1, w3, w2_
                 )
 
         chunks = S // CHUNK
-        act = [keep.tile([P, CHUNK, PACK], F32, name=f"act{c}") for c in range(chunks)]
         h_bf = keep.tile([P, S * PACK], BF16, name="h_bf", align_bytes=64)
-        h_codes = keep.tile([P, S], U32, name="h_codes", align_bytes=64)
         h_scales = keep.tile([P, S], U8, name="h_scales", align_bytes=64)
         y = [keep.tile([P, S], F32, name=f"y{m}") for m in range(N // P)]
+        act_slot = ["act0", "act1", "act2", "act3", "act4", "w3_bf1", "act0", "act1"]
+        act = {}
 
         def h_of(c):
             return h_bf[:, c * CHUNK * PACK : (c + 1) * CHUNK * PACK].rearrange("p (n t) -> p n t", t=PACK)
@@ -116,36 +116,44 @@ def tile_picked_route2_glusilu_p_kernel(tc, x_words, x_scales, gate, w1, w3, w2_
         def gate_branch(c):
             bank = psum_a.tile([P, PACK, CHUNK], F32, name="bank_a", tag="ring")
             first_product(bank, w1_codes, w1_scales, c)
+            return bank
+
+        def activate(c, bank):
+            act[c] = keep.tile([P, CHUNK, PACK], F32, name=f"act{c}", tag=act_slot[c], align_bytes=64)
             nc.scalar.activation(act[c][:], bank[:].rearrange("p t n -> p n t"), SILU)
 
-        def hidden(c):
+        def linear_branch(c):
             bank = psum_b.tile([P, PACK, CHUNK], F32, name="bank_b")
             first_product(bank, w3_codes, w3_scales, c)
+            return bank
+
+        def hidden(c):
+            bank = linear_branch(c)
             nc.vector.tensor_tensor(h_of(c), bank[:].rearrange("p t n -> p n t"), act[c][:], MULT)
 
         def hidden_aside(c):
-            bank = psum_a.tile([P, PACK, CHUNK], F32, name="bank_c", tag="ring")
-            first_product(bank, w3_codes, w3_scales, c)
-            lin = keep.tile([P, CHUNK, PACK], F32, name=f"lin{c}")
+            bank = linear_branch(c)
+            lin = keep.tile([P, CHUNK, PACK], F32, name=f"lin{c}", tag=f"lin{c}", align_bytes=64)
             nc.scalar.copy(lin[:], bank[:].rearrange("p t n -> p n t"))
             nc.gpsimd.tensor_tensor(h_of(c), lin[:], act[c][:], MULT)
 
-        def second_product(j0, j1):
+        def quantise_hidden(j0, j1):
             nc.vector.quantize_mx(
                 out=h_codes[:, j0:j1].bitcast(FP8X4), scales=h_scales[:, j0:j1], in_=h_bf[:, PACK * j0 : PACK * j1]
             )
-            for m in range(N // P):
-                bank = psum_a.tile([P, j1 - j0], F32, name="bank_y", tag="ring")
-                nc.tensor.matmul_mx(
-                    out=bank[:],
-                    lhsT=w2w[:, 2 * m * P : 2 * (m + 1) * P].bitcast(FP4X4),
-                    lhsT_scale=w2s[:, m * P : (m + 1) * P],
-                    rhs=h_codes[:, j0:j1].bitcast(FP8X4),
-                    rhs_scale=h_scales[:, j0:j1],
-                    start=True,
-                    stop=True,
-                )
-                nc.scalar.copy(y[m][:, j0:j1], bank[:])
+
+        def second_product(m, j0, j1):
+            bank = psum_a.tile([P, j1 - j0], F32, name="bank_y", tag="ring")
+            nc.tensor.matmul_mx(
+                out=bank[:],
+                lhsT=w2w[:, 2 * m * P : 2 * (m + 1) * P].bitcast(FP4X4),
+                lhsT_scale=w2s[:, m * P : (m + 1) * P],
+                rhs=h_codes[:, j0:j1].bitcast(FP8X4),
+                rhs_scale=h_scales[:, j0:j1],
+                start=True,
+                stop=True,
+            )
+            nc.scalar.copy(y[m][:, j0:j1], bank[:])
 
         def put(m, j0, j1):
             nc.vector.tensor_tensor(
@@ -157,21 +165,29 @@ def tile_picked_route2_glusilu_p_kernel(tc, x_words, x_scales, gate, w1, w3, w2_
         for u in range(2):
             cols = slice(u * H // 2, (u + 1) * H // 2)
             nc.vector.quantize_mx(out=w3_codes[:, cols].bitcast(FP8X4), scales=w3_scales[:, cols], in_=w3_bf[u][:])
-        for c in range(AHEAD):
-            gate_branch(c)
-        for c in range(chunks - SHARED):
+        for c in range(5):
+            activate(c, gate_branch(c))
+        late = {c: gate_branch(c) for c in range(5, chunks)}
+        hidden(0)
+        hidden_aside(2)
+        hidden(1)
+        hidden(4)
+        hidden_aside(3)
+        h_codes = keep.tile([P, S], U32, name="h_codes", tag="act4", align_bytes=64)
+        quantise_hidden(0, PAIR)
+        second_product(0, 0, PAIR)
+        for c in range(5, chunks):
+            activate(c, late[c])
             hidden(c)
-            if c + AHEAD < chunks:
-                gate_branch(c + AHEAD)
-            if c + AHEAD == chunks - 1:
-                for aside in range(chunks - SHARED, chunks):
-                    hidden_aside(aside)
-            if c >= 2 and c % 2 == 0:
-                second_product((c - 2) * CHUNK, c * CHUNK)
+        pieces = ((PAIR, S // 2), (S // 2, S))
+        for j0, j1 in pieces:
+            quantise_hidden(j0, j1)
+        for j0, j1 in pieces:
+            second_product(0, j0, j1)
+        for j0 in (0, S // 2):
+            second_product(1, j0, j0 + S // 2)
         put(0, 0, PAIR)
-        second_product(S // 2, S)
-        put(0, PAIR, S // 2)
-        put(0, S // 2, S)
+        put(0, PAIR, S)
         nc.sync.dma_start(out[0:P, :], windows[0][:])
         put(1, 0, S)
         nc.sync.dma_start(out[P : 2 * P, 0 : U // 2], windows[1][:, 0 : U // 2])

@@ -175,20 +175,20 @@ def tile_picked_route2_glusilu_p_kernel(tc, x_words, x_scales, gate, w1, w3, w2_
         hidden_aside(3)
         h_codes = keep.tile([P, S], U32, name="h_codes", tag="act4", align_bytes=64)
         quantise_hidden(0, PAIR)
-        second_product(0, 0, PAIR)
+        for m in range(N // P):
+            second_product(m, 0, PAIR)
         for c in range(5, chunks):
             activate(c, late[c])
             hidden(c)
         pieces = ((PAIR, S // 2), (S // 2, S))
         for j0, j1 in pieces:
             quantise_hidden(j0, j1)
-        for j0, j1 in pieces:
-            second_product(0, j0, j1)
-        for j0 in (0, S // 2):
-            second_product(1, j0, j0 + S // 2)
-        put(0, 0, PAIR)
-        put(0, PAIR, S)
+        for m in range(N // P):
+            for j0, j1 in pieces:
+                second_product(m, j0, j1)
+        for j0, j1 in ((0, PAIR), (PAIR, S)):
+            for m in range(N // P):
+                put(m, j0, j1)
         nc.sync.dma_start(out[0:P, :], windows[0][:])
-        put(1, 0, S)
         nc.sync.dma_start(out[P : 2 * P, 0 : U // 2], windows[1][:, 0 : U // 2])
         nc.scalar.dma_start(out[P : 2 * P, U // 2 : U], windows[1][:, U // 2 : U])

@@ -21,7 +21,7 @@ PACK = 4
 CHUNK = 128
 PAIR = 2 * CHUNK
 GATHER = 512
-ASIDE = (2, 3)
+LATE_SHARE = 96
 
 
 def tile_picked_route2_glusilu_p_kernel(tc, x_words, x_scales, gate, w1, w3, w2_words, w2_scales, offs, dst, out):
@@ -104,14 +104,18 @@ def tile_picked_route2_glusilu_p_kernel(tc, x_words, x_scales, gate, w1, w3, w2_
                 )
 
         chunks = S // CHUNK
-        h_bf = keep.tile([P, S * PACK], BF16, name="h_bf", align_bytes=64)
+        h_bf = keep.tile([P, (S - PAIR) * PACK], BF16, name="h_bf", align_bytes=64)
         h_scales = keep.tile([P, S], U8, name="h_scales", align_bytes=64)
         y = [keep.tile([P, S], F32, name=f"y{m}") for m in range(N // P)]
-        act_slot = ["act0", "act1", "act2", "act3", "act4", "w3_bf1", "act0", "act1"]
+        act_slot = ["act0", "act1", "act1", "w3_bf1", "act4", "act5", "act6", "act0"]
         act = {}
 
+        def h_columns(j0, j1):
+            back = PAIR if j0 >= PAIR else 0
+            return h_bf[:, (j0 - back) * PACK : (j1 - back) * PACK]
+
         def h_of(c):
-            return h_bf[:, c * CHUNK * PACK : (c + 1) * CHUNK * PACK].rearrange("p (n t) -> p n t", t=PACK)
+            return h_columns(c * CHUNK, (c + 1) * CHUNK).rearrange("p (n t) -> p n t", t=PACK)
 
         def gate_branch(c):
             bank = psum_a.tile([P, PACK, CHUNK], F32, name="bank_a", tag="ring")
@@ -131,15 +135,14 @@ def tile_picked_route2_glusilu_p_kernel(tc, x_words, x_scales, gate, w1, w3, w2_
             bank = linear_branch(c)
             nc.vector.tensor_tensor(h_of(c), bank[:].rearrange("p t n -> p n t"), act[c][:], MULT)
 
-        def hidden_aside(c):
-            bank = linear_branch(c)
-            lin = keep.tile([P, CHUNK, PACK], F32, name=f"lin{c}", tag=f"lin{c}", align_bytes=64)
-            nc.scalar.copy(lin[:], bank[:].rearrange("p t n -> p n t"))
-            nc.gpsimd.tensor_tensor(h_of(c), lin[:], act[c][:], MULT)
+        def copy_aside(c, bank, n):
+            lin = keep.tile([P, n, PACK], F32, name=f"lin{c}", align_bytes=64)
+            nc.scalar.copy(lin[:], bank[:, :, 0:n].rearrange("p t n -> p n t"))
+            return lin
 
         def quantise_hidden(j0, j1):
             nc.vector.quantize_mx(
-                out=h_codes[:, j0:j1].bitcast(FP8X4), scales=h_scales[:, j0:j1], in_=h_bf[:, PACK * j0 : PACK * j1]
+                out=h_codes[:, j0:j1].bitcast(FP8X4), scales=h_scales[:, j0:j1], in_=h_columns(j0, j1)
             )
 
         def second_product(m, j0, j1):
@@ -165,22 +168,34 @@ def tile_picked_route2_glusilu_p_kernel(tc, x_words, x_scales, gate, w1, w3, w2_
         for u in range(2):
             cols = slice(u * H // 2, (u + 1) * H // 2)
             nc.vector.quantize_mx(out=w3_codes[:, cols].bitcast(FP8X4), scales=w3_scales[:, cols], in_=w3_bf[u][:])
-        for c in range(5):
+        for c in (0, 1, 4, 5, 6):
             activate(c, gate_branch(c))
-        late = {c: gate_branch(c) for c in range(5, chunks)}
+        late = {c: gate_branch(c) for c in (3, 7, 2)}
         hidden(0)
-        hidden_aside(2)
+        lin = copy_aside(4, linear_branch(4), CHUNK)
+        nc.gpsimd.tensor_tensor(h_of(4), lin[:], act[4][:], MULT)
         hidden(1)
-        hidden(4)
-        hidden_aside(3)
-        h_codes = keep.tile([P, S], U32, name="h_codes", tag="act4", align_bytes=64)
+        hidden(5)
+        hidden(6)
+        activate(3, late[3])
+        shared_bank = linear_branch(3)
+        lin = copy_aside(3, shared_bank, LATE_SHARE)
+        h_codes = keep.tile([P, S], U32, name="h_codes", tag="act5", align_bytes=64)
         quantise_hidden(0, PAIR)
+        nc.gpsimd.tensor_tensor(h_of(3)[:, 0:LATE_SHARE], lin[:], act[3][:, 0:LATE_SHARE], MULT)
         for m in range(N // P):
             second_product(m, 0, PAIR)
-        for c in range(5, chunks):
-            activate(c, late[c])
-            hidden(c)
-        pieces = ((PAIR, S // 2), (S // 2, S))
+        activate(7, late[7])
+        hidden(7)
+        nc.vector.tensor_tensor(
+            h_of(3)[:, LATE_SHARE:CHUNK],
+            shared_bank[:, :, LATE_SHARE:CHUNK].rearrange("p t n -> p n t"),
+            act[3][:, LATE_SHARE:CHUNK],
+            MULT,
+        )
+        activate(2, late[2])
+        hidden(2)
+        pieces = ((S // 2, S), (PAIR, S // 2))
         for j0, j1 in pieces:
             quantise_hidden(j0, j1)
         for m in range(N // P):

@@ -36,19 +36,24 @@ def tile_picked_route2_glusilu_p_kernel(tc, x_words, x_scales, gate, w1, w3, w2_
         dst_sb = keep.tile([P, S // 16], U16, name="dst_sb")
         xs = reuse.tile([P, T], U8, name="xs", offset=3 * T // 2, align_bytes=64)
         w1_raw = keep.tile([P, PACK, H], F32, name="w1_raw", tag="early", align_bytes=64)
-        xw = keep.tile([P, T], U32, name="xw", tag="xw_slot", align_bytes=64)
+        seed = reuse.tile([P, 32], F32, name="seed", offset=4 * T, align_bytes=64)
         zeros = keep.tile([P, 32], F32, name="zeros")
         x_planes = keep.tile([P, S], U8, name="x_planes", align_bytes=64)
         window1 = keep.tile([P, U], F32, name="window1")
 
-        nc.sync.dma_start(xs[112:P, :].bitcast(I32), x_scales[0].bitcast(I32))
+        w1_rows = w1.rearrange("(p j) c -> p j c", j=PACK)
+        nc.sync.dma_start(w1_raw[:, 0:2, :], w1_rows[:, 0:2, :])
         nc.sync.dma_start(offs_sb[:], offs)
-        nc.sync.dma_start(w1_raw[:], w1.rearrange("(p j) c -> p j c", j=PACK))
-        nc.sync.dma_start(xw[:].bitcast(I32), x_words[0].rearrange("p n t -> p (n t)").bitcast(I32))
         nc.sync.dma_start(dst_sb[:], dst)
-        nc.vector.memset(zeros[:], 0.0)
+        nc.vector.memset(seed[:], 0.0)
+        nc.vector.memset(w1_raw[:, 2, 0:32], 0.0)
+        nc.vector.memset(xs[:].bitcast(I32), 0)
+        nc.vector.tensor_tensor(zeros[:], seed[:], w1_raw[:, 2, 0:32], MULT)
+        nc.sync.dma_start(xs[32:96:4, :].bitcast(I32), x_scales[0].bitcast(I32))
+        nc.sync.dma_start(w1_raw[:, 2:4, :], w1_rows[:, 2:4, :])
+        xw = reuse.tile([P, T], U32, name="xw", offset=4 * T, align_bytes=64)
+        nc.sync.dma_start(xw[:].bitcast(I32), x_words[0].rearrange("p n t -> p (n t)").bitcast(I32))
         nc.scalar.activation(window1[:], zeros[:, 0:1].to_broadcast([P, U]), SILU)
-        nc.vector.memset(xs[0:112, :].bitcast(I32), 0)
         nc.vector.memset(x_planes[:].bitcast(I32), 0)
 
         def dealt(raw, grouped, t0, t1):
@@ -69,7 +74,7 @@ def tile_picked_route2_glusilu_p_kernel(tc, x_words, x_scales, gate, w1, w3, w2_
         nc.vector.tensor_copy(picked_s[:], xs[:].indirect(offs_sb[:]))
         for r in range(4):
             nc.sync.dma_start(
-                x_planes[32 * r : 32 * r + 4, :].bitcast(I32), picked_s[112 + 4 * r : 116 + 4 * r, :].bitcast(I32)
+                x_planes[32 * r : 32 * r + 4, :].bitcast(I32), picked_s[32 + 16 * r : 48 + 16 * r : 4, :].bitcast(I32)
             )
         w3_raw = reuse.tile([P, PACK, H], F32, name="w3_raw", offset=0, align_bytes=64)
         nc.sync.dma_start(w3_raw[:], w3.rearrange("(p j) c -> p j c", j=PACK))
@@ -87,7 +92,7 @@ def tile_picked_route2_glusilu_p_kernel(tc, x_words, x_scales, gate, w1, w3, w2_
         for g in range(S // GATHER):
             cols = slice(g * GATHER // 16, (g + 1) * GATHER // 16)
             nc.vector.tensor_copy(picked_w[g][:], xw[:].indirect(offs_sb[:, cols]))
-        gate_row = keep.tile([P, S], F32, name="gate_row", tag="xw_slot", align_bytes=64)
+        gate_row = reuse.tile([P, S], F32, name="gate_row", offset=4 * T, align_bytes=64)
         nc.sync.dma_start(gate_row[:], gate)
 
         def first_product(bank, codes, scales, c):

@@ -21,7 +21,6 @@ PACK = 4
 CHUNK = 128
 PAIR = 2 * CHUNK
 GATHER = 512
-LATE_SHARE = 96
 
 
 def tile_picked_route2_glusilu_p_kernel(tc, x_words, x_scales, gate, w1, w3, w2_words, w2_scales, offs, dst, out):
@@ -108,52 +107,46 @@ def tile_picked_route2_glusilu_p_kernel(tc, x_words, x_scales, gate, w1, w3, w2_
                     stop=True,
                 )
 
-        chunks = S // CHUNK
-        h_bf = keep.tile([P, (S - PAIR) * PACK], BF16, name="h_bf", align_bytes=64)
+        h_bf = keep.tile([P, 5 * CHUNK * PACK], BF16, name="h_bf", align_bytes=64)
+        h_codes = keep.tile([P, S], U32, name="h_codes", align_bytes=64)
         h_scales = keep.tile([P, S], U8, name="h_scales", align_bytes=64)
-        y = [keep.tile([P, S], F32, name=f"y{m}") for m in range(N // P)]
-        act_slot = ["act0", "act1", "act1", "w3_bf1", "act4", "act5", "act6", "act0"]
-        act = {}
+        act = [keep.tile([P, PAIR, PACK], F32, name=f"act{u}", align_bytes=64) for u in range(S // PAIR)]
+        lin = {u: keep.tile([P, PAIR, PACK], F32, name=f"lin{u}", tag=f"lin{u}", align_bytes=64) for u in (2, 3)}
 
         def h_columns(j0, j1):
-            back = PAIR if j0 >= PAIR else 0
+            back = 3 * CHUNK if j0 >= S // 2 else 0
             return h_bf[:, (j0 - back) * PACK : (j1 - back) * PACK]
 
-        def h_of(c):
-            return h_columns(c * CHUNK, (c + 1) * CHUNK).rearrange("p (n t) -> p n t", t=PACK)
+        def h_of(j0, j1):
+            return h_columns(j0, j1).rearrange("p (n t) -> p n t", t=PACK)
 
-        def gate_branch(c):
+        def half(tile, c):
+            return tile[:, (c % 2) * CHUNK : (c % 2 + 1) * CHUNK, :]
+
+        def activate(c):
             bank = psum_a.tile([P, PACK, CHUNK], F32, name="bank_a", tag="ring")
             first_product(bank, w1_codes, w1_scales, c)
-            return bank
-
-        def activate(c, bank):
-            act[c] = keep.tile([P, CHUNK, PACK], F32, name=f"act{c}", tag=act_slot[c], align_bytes=64)
-            nc.scalar.activation(act[c][:], bank[:].rearrange("p t n -> p n t"), SILU)
+            nc.scalar.activation(half(act[c // 2], c), bank[:].rearrange("p t n -> p n t"), SILU)
 
         def linear_branch(c):
             bank = psum_b.tile([P, PACK, CHUNK], F32, name="bank_b")
             first_product(bank, w3_codes, w3_scales, c)
-            return bank
+            return bank[:].rearrange("p t n -> p n t")
 
         def hidden(c):
-            bank = linear_branch(c)
-            nc.vector.tensor_tensor(h_of(c), bank[:].rearrange("p t n -> p n t"), act[c][:], MULT)
+            nc.vector.tensor_tensor(h_of(c * CHUNK, (c + 1) * CHUNK), linear_branch(c), half(act[c // 2], c), MULT)
 
-        def copy_aside(c, bank, n):
-            lin = keep.tile([P, n, PACK], F32, name=f"lin{c}", align_bytes=64)
-            nc.scalar.copy(lin[:], bank[:, :, 0:n].rearrange("p t n -> p n t"))
-            return lin
+        def copy_aside(c):
+            nc.scalar.copy(half(lin[c // 2], c), linear_branch(c))
 
         def quantise_hidden(j0, j1):
             nc.vector.quantize_mx(
                 out=h_codes[:, j0:j1].bitcast(FP8X4), scales=h_scales[:, j0:j1], in_=h_columns(j0, j1)
             )
 
-        def second_product(m, j0, j1):
-            bank = psum_a.tile([P, j1 - j0], F32, name="bank_y", tag="ring")
+        def second_product(into, m, j0, j1):
             nc.tensor.matmul_mx(
-                out=bank[:],
+                out=into,
                 lhsT=w2w[:, 2 * m * P : 2 * (m + 1) * P].bitcast(FP4X4),
                 lhsT_scale=w2s[:, m * P : (m + 1) * P],
                 rhs=h_codes[:, j0:j1].bitcast(FP8X4),
@@ -161,54 +154,62 @@ def tile_picked_route2_glusilu_p_kernel(tc, x_words, x_scales, gate, w1, w3, w2_
                 start=True,
                 stop=True,
             )
-            nc.scalar.copy(y[m][:, j0:j1], bank[:])
 
-        def put(m, j0, j1):
-            nc.vector.tensor_tensor(
-                windows[m][:].indirect(dst_sb[:, j0 // 16 : j1 // 16]), y[m][:, j0:j1], gate_row[:, j0:j1], MULT
-            )
+        def places(m, j0, j1):
+            return windows[m][:].indirect(dst_sb[:, j0 // 16 : j1 // 16])
 
         for u in range(2):
             nc.vector.tensor_copy(*dealt(w3_raw, w3_bf[u], 2 * u, 2 * u + 2))
         for u in range(2):
             cols = slice(u * H // 2, (u + 1) * H // 2)
             nc.vector.quantize_mx(out=w3_codes[:, cols].bitcast(FP8X4), scales=w3_scales[:, cols], in_=w3_bf[u][:])
-        for c in (0, 1, 4, 5, 6):
-            activate(c, gate_branch(c))
-        late = {c: gate_branch(c) for c in (3, 7, 2)}
-        hidden(0)
-        lin = copy_aside(4, linear_branch(4), CHUNK)
-        nc.gpsimd.tensor_tensor(h_of(4), lin[:], act[4][:], MULT)
-        hidden(1)
-        hidden(5)
-        hidden(6)
-        activate(3, late[3])
-        shared_bank = linear_branch(3)
-        lin = copy_aside(3, shared_bank, LATE_SHARE)
-        h_codes = keep.tile([P, S], U32, name="h_codes", tag="act5", align_bytes=64)
+        def weigh(name, bank, j0, j1):
+            weighed = keep.tile([P, j1 - j0], F32, name=name)
+            nc.vector.tensor_tensor(weighed[:], bank, gate_row[:, j0:j1], MULT)
+            return weighed
+
+        for c in range(6):
+            activate(c)
+        for c in range(2):
+            hidden(c)
+        third = linear_branch(2)
+        cut = PAIR + CHUNK // 2
+        nc.vector.tensor_tensor(h_of(PAIR, cut), third[:, 0 : CHUNK // 2], act[1][:, 0 : CHUNK // 2], MULT)
         quantise_hidden(0, PAIR)
-        nc.gpsimd.tensor_tensor(h_of(3)[:, 0:LATE_SHARE], lin[:], act[3][:, 0:LATE_SHARE], MULT)
-        for m in range(N // P):
-            second_product(m, 0, PAIR)
-        activate(7, late[7])
-        hidden(7)
-        nc.vector.tensor_tensor(
-            h_of(3)[:, LATE_SHARE:CHUNK],
-            shared_bank[:, :, LATE_SHARE:CHUNK].rearrange("p t n -> p n t"),
-            act[3][:, LATE_SHARE:CHUNK],
-            MULT,
-        )
-        activate(2, late[2])
-        hidden(2)
-        pieces = ((S // 2, S), (PAIR, S // 2))
-        for j0, j1 in pieces:
-            quantise_hidden(j0, j1)
-        for m in range(N // P):
-            for j0, j1 in pieces:
-                second_product(m, j0, j1)
-        for j0, j1 in ((0, PAIR), (PAIR, S)):
-            for m in range(N // P):
-                put(m, j0, j1)
+        first_bank = psum_a.tile([P, PAIR], F32, name="first_bank", tag="ring")
+        second_product(first_bank[:], 0, 0, PAIR)
+        nc.vector.tensor_tensor(h_of(cut, 3 * CHUNK), third[:, CHUNK // 2 : CHUNK], act[1][:, CHUNK // 2 : CHUNK], MULT)
+        hidden(3)
+        first = weigh("first", first_bank[:], 0, PAIR)
+        quantise_hidden(PAIR, S // 2)
+        for c in (4, 5):
+            copy_aside(c)
+        for c in (6, 7):
+            activate(c)
+        for c in (6, 7):
+            copy_aside(c)
+        for u in (2, 3):
+            nc.gpsimd.tensor_tensor(h_of(u * PAIR, (u + 1) * PAIR), lin[u][:], act[u][:], MULT)
+        nc.vector.tensor_copy(places(0, 0, PAIR), first[:])
+        both_bank = psum_a.tile([P, 2, PAIR], F32, name="both_bank", tag="ring")
+        second_product(both_bank[:, 0, :], 1, 0, PAIR)
+        second_product(both_bank[:, 1, :], 0, PAIR, S // 2)
+        held_bank = psum_a.tile([P, PAIR], F32, name="held_bank", tag="ring")
+        second_product(held_bank[:], 1, PAIR, S // 2)
+        second = weigh("second", both_bank[:, 0, :], 0, PAIR)
+        third_y = weigh("third_y", both_bank[:, 1, :], PAIR, S // 2)
+        nc.vector.tensor_copy(places(1, 0, PAIR), second[:])
+        nc.vector.tensor_copy(places(0, PAIR, S // 2), third_y[:])
+        quantise_hidden(S // 2, S)
+        held = keep.tile([P, PAIR], F32, name="held", tag="lin3", align_bytes=64)
+        nc.scalar.copy(held[:], held_bank[:])
+        nc.vector.tensor_tensor(places(1, PAIR, S // 2), held[:], gate_row[:, PAIR : S // 2], MULT)
+        for m in range(2):
+            bank = psum_b.tile([P, S // 2], F32, name="bank_b")
+            second_product(bank[:], m, S // 2, S)
+            last = keep.tile([P, S // 2], F32, name=f"last{m}")
+            nc.scalar.copy(last[:], bank[:])
+            nc.vector.tensor_tensor(places(m, S // 2, S), last[:], gate_row[:, S // 2 : S], MULT)
         nc.sync.dma_start(out[0:P, :], windows[0][:])
         nc.sync.dma_start(out[P : 2 * P, 0 : U // 2], windows[1][:, 0 : U // 2])
         nc.scalar.dma_start(out[P : 2 * P, U // 2 : U], windows[1][:, U // 2 : U])

@@ -21,6 +21,7 @@ PACK = 4
 CHUNK = 128
 PAIR = 2 * CHUNK
 GATHER = 512
+HELP = 64
 
 
 def tile_picked_route2_glusilu_p_kernel(tc, x_words, x_scales, gate, w1, w3, w2_words, w2_scales, offs, dst, out):
@@ -28,14 +29,13 @@ def tile_picked_route2_glusilu_p_kernel(tc, x_words, x_scales, gate, w1, w3, w2_
     with ExitStack() as ctx:
         keep = ctx.enter_context(tc.tile_pool(name="keep", bufs=1))
         reuse = ctx.enter_context(tc.tile_pool(name="reuse", bufs=1))
-        psum_a = ctx.enter_context(tc.psum_pool(name="psum_a", bufs=4))
-        psum_b = ctx.enter_context(tc.psum_pool(name="psum_b", bufs=4))
+        psum = ctx.enter_context(tc.psum_pool(name="psum", bufs=1))
 
         offs_sb = keep.tile([P, S // 16], U16, name="offs_sb")
         dst_sb = keep.tile([P, S // 16], U16, name="dst_sb")
-        xs = reuse.tile([P, T], U8, name="xs", offset=3 * T // 2, align_bytes=64)
-        w1_raw = keep.tile([P, PACK, H], F32, name="w1_raw", tag="early", align_bytes=64)
-        seed = reuse.tile([P, 32], F32, name="seed", offset=4 * T, align_bytes=64)
+        xs = reuse.tile([P, T], U8, name="xs", offset=2 * T, align_bytes=64)
+        w1_raw = reuse.tile([P, PACK, H], F32, name="w1_raw", offset=9 * T, align_bytes=64)
+        seed = reuse.tile([P, 32], F32, name="seed", offset=9 * T // 2, align_bytes=64)
         zeros = keep.tile([P, 32], F32, name="zeros")
         x_planes = keep.tile([P, S], U8, name="x_planes", align_bytes=64)
         window1 = keep.tile([P, U], F32, name="window1")
@@ -50,14 +50,14 @@ def tile_picked_route2_glusilu_p_kernel(tc, x_words, x_scales, gate, w1, w3, w2_
         nc.vector.tensor_tensor(zeros[:], seed[:], w1_raw[:, 2, 0:32], MULT)
         nc.sync.dma_start(xs[32:96:4, :].bitcast(I32), x_scales[0].bitcast(I32))
         nc.sync.dma_start(w1_raw[:, 2:4, :], w1_rows[:, 2:4, :])
-        xw = reuse.tile([P, T], U32, name="xw", offset=4 * T, align_bytes=64)
+        xw = reuse.tile([P, T], U32, name="xw", offset=9 * T // 2, align_bytes=64)
         nc.sync.dma_start(xw[:].bitcast(I32), x_words[0].rearrange("p n t -> p (n t)").bitcast(I32))
         nc.scalar.activation(window1[:], zeros[:, 0:1].to_broadcast([P, U]), SILU)
         nc.vector.memset(x_planes[:].bitcast(I32), 0)
 
-        def dealt(raw, grouped, t0, t1):
+        def dealt(raw, grouped, t0, t1, j0, j1):
             src = raw[:].rearrange("p j (m t) -> p m t j", t=PACK)[:, :, t0:t1, :]
-            to = grouped[:].rearrange("p (t m j) -> p m t j", m=P, j=PACK)
+            to = grouped[:].rearrange("p (t m j) -> p m t j", m=P, j=PACK)[:, :, :, j0:j1]
             return to, src
 
         w1_bf = keep.tile([P, PACK * H], BF16, name="w1_bf", tag="w1_bf", align_bytes=64)
@@ -66,7 +66,7 @@ def tile_picked_route2_glusilu_p_kernel(tc, x_words, x_scales, gate, w1, w3, w2_
         w3_codes = keep.tile([P, H], U32, name="w3_codes", align_bytes=64)
         w3_scales = keep.tile([P, H], U8, name="w3_scales", align_bytes=64)
 
-        nc.scalar.copy(*dealt(w1_raw, w1_bf, 0, PACK))
+        nc.scalar.copy(*dealt(w1_raw, w1_bf, 0, PACK, 0, PACK))
 
         picked_w = [keep.tile([P, GATHER], U32, name=f"picked_w{g}", align_bytes=64) for g in range(S // GATHER)]
         picked_s = keep.tile([P, S], U8, name="picked_s", align_bytes=64)
@@ -75,12 +75,17 @@ def tile_picked_route2_glusilu_p_kernel(tc, x_words, x_scales, gate, w1, w3, w2_
             nc.sync.dma_start(
                 x_planes[32 * r : 32 * r + 4, :].bitcast(I32), picked_s[32 + 16 * r : 48 + 16 * r : 4, :].bitcast(I32)
             )
-        w3_raw = reuse.tile([P, PACK, H], F32, name="w3_raw", offset=0, align_bytes=64)
-        nc.sync.dma_start(w3_raw[:], w3.rearrange("(p j) c -> p j c", j=PACK))
-        window0 = reuse.tile([P, U], F32, name="window0", offset=2 * T, align_bytes=64)
+        w3_rows = w3.rearrange("(p j) c -> p j c", j=PACK)
+        w3_raw = [
+            reuse.tile([P, 2, H], F32, name="w3_raw0", offset=3 * T // 2, align_bytes=64),
+            reuse.tile([P, 2, H], F32, name="w3_raw1", offset=9 * T, align_bytes=64),
+        ]
+        for v in range(2):
+            nc.sync.dma_start(w3_raw[v][:], w3_rows[:, 2 * v : 2 * v + 2, :])
+        window0 = reuse.tile([P, U], F32, name="window0", offset=5 * T // 2, align_bytes=64)
         nc.vector.memset(window0[:], 0.0)
         windows = [window0, window1]
-        w2w = keep.tile([P, 2 * N], U8, name="w2w", tag="early", align_bytes=64)
+        w2w = reuse.tile([P, 2 * N], U8, name="w2w", offset=10 * T, align_bytes=64)
         nc.sync.dma_start(w2w[:].bitcast(I32), w2_words[0].bitcast(I32))
         w1_scales = keep.tile([P, H], U8, name="w1_scales", align_bytes=64)
         nc.vector.quantize_mx(out=w1_codes[:].bitcast(FP8X4), scales=w1_scales[:], in_=w1_bf[:])
@@ -91,7 +96,7 @@ def tile_picked_route2_glusilu_p_kernel(tc, x_words, x_scales, gate, w1, w3, w2_
         for g in range(S // GATHER):
             cols = slice(g * GATHER // 16, (g + 1) * GATHER // 16)
             nc.vector.tensor_copy(picked_w[g][:], xw[:].indirect(offs_sb[:, cols]))
-        gate_row = reuse.tile([P, S], F32, name="gate_row", offset=4 * T, align_bytes=64)
+        gate_row = reuse.tile([P, S], F32, name="gate_row", offset=9 * T // 2, align_bytes=64)
         nc.sync.dma_start(gate_row[:], gate)
 
         def first_product(bank, codes, scales, c):
@@ -107,37 +112,48 @@ def tile_picked_route2_glusilu_p_kernel(tc, x_words, x_scales, gate, w1, w3, w2_
                     stop=True,
                 )
 
-        h_bf = keep.tile([P, 5 * CHUNK * PACK], BF16, name="h_bf", align_bytes=64)
+        half = S // 2
+        h_bf = keep.tile([P, (S - CHUNK) * PACK], BF16, name="h_bf", align_bytes=64)
         h_codes = keep.tile([P, S], U32, name="h_codes", align_bytes=64)
         h_scales = keep.tile([P, S], U8, name="h_scales", align_bytes=64)
-        act = [keep.tile([P, PAIR, PACK], F32, name=f"act{u}", align_bytes=64) for u in range(S // PAIR)]
-        lin = {u: keep.tile([P, PAIR, PACK], F32, name=f"lin{u}", tag=f"lin{u}", align_bytes=64) for u in (2, 3)}
+        act_early = reuse.tile([P, half, PACK], F32, name="act_early", offset=T // 2, align_bytes=64)
+        act_late = keep.tile([P, half, PACK], F32, name="act_late", align_bytes=64)
+        lin = keep.tile([P, half, PACK], F32, name="lin", tag="lin", align_bytes=64)
+
+        def act(j0, j1):
+            return act_early[:, j0:j1, :] if j0 < half else act_late[:, j0 - half : j1 - half, :]
 
         def h_columns(j0, j1):
-            back = 3 * CHUNK if j0 >= S // 2 else 0
+            back = CHUNK if j0 >= half else 0
             return h_bf[:, (j0 - back) * PACK : (j1 - back) * PACK]
 
         def h_of(j0, j1):
             return h_columns(j0, j1).rearrange("p (n t) -> p n t", t=PACK)
 
-        def half(tile, c):
-            return tile[:, (c % 2) * CHUNK : (c % 2 + 1) * CHUNK, :]
-
         def activate(c):
-            bank = psum_a.tile([P, PACK, CHUNK], F32, name="bank_a", tag="ring")
+            bank = psum.tile([P, PACK, CHUNK], F32, name=f"gate_bank{c}", tag=f"bank{c}")
             first_product(bank, w1_codes, w1_scales, c)
-            nc.scalar.activation(half(act[c // 2], c), bank[:].rearrange("p t n -> p n t"), SILU)
+            nc.scalar.activation(act(c * CHUNK, (c + 1) * CHUNK), bank[:].rearrange("p t n -> p n t"), SILU)
+
+        linear = {}
 
         def linear_branch(c):
-            bank = psum_b.tile([P, PACK, CHUNK], F32, name="bank_b")
+            bank = psum.tile([P, PACK, CHUNK], F32, name=f"linear_bank{c}", tag=f"bank{(c + 4) % 8}")
             first_product(bank, w3_codes, w3_scales, c)
-            return bank[:].rearrange("p t n -> p n t")
+            linear[c] = bank[:].rearrange("p t n -> p n t")
 
-        def hidden(c):
-            nc.vector.tensor_tensor(h_of(c * CHUNK, (c + 1) * CHUNK), linear_branch(c), half(act[c // 2], c), MULT)
+        def in_bank(j0, j1):
+            c = j0 // CHUNK
+            return linear[c][:, j0 - c * CHUNK : j1 - c * CHUNK]
 
-        def copy_aside(c):
-            nc.scalar.copy(half(lin[c // 2], c), linear_branch(c))
+        def hidden(j0, j1):
+            nc.vector.tensor_tensor(h_of(j0, j1), in_bank(j0, j1), act(j0, j1), MULT)
+
+        def copy_aside(j0, j1):
+            nc.scalar.copy(lin[:, j0 - half : j1 - half, :], in_bank(j0, j1))
+
+        def hidden_aside(j0, j1):
+            nc.gpsimd.tensor_tensor(h_of(j0, j1), lin[:, j0 - half : j1 - half, :], act(j0, j1), MULT)
 
         def quantise_hidden(j0, j1):
             nc.vector.quantize_mx(
@@ -158,58 +174,58 @@ def tile_picked_route2_glusilu_p_kernel(tc, x_words, x_scales, gate, w1, w3, w2_
         def places(m, j0, j1):
             return windows[m][:].indirect(dst_sb[:, j0 // 16 : j1 // 16])
 
-        for u in range(2):
-            nc.vector.tensor_copy(*dealt(w3_raw, w3_bf[u], 2 * u, 2 * u + 2))
-        for u in range(2):
-            cols = slice(u * H // 2, (u + 1) * H // 2)
-            nc.vector.quantize_mx(out=w3_codes[:, cols].bitcast(FP8X4), scales=w3_scales[:, cols], in_=w3_bf[u][:])
         def weigh(name, bank, j0, j1):
             weighed = keep.tile([P, j1 - j0], F32, name=name)
             nc.vector.tensor_tensor(weighed[:], bank, gate_row[:, j0:j1], MULT)
             return weighed
 
-        for c in range(6):
+        for v, engine_copy in enumerate((nc.scalar.copy, nc.vector.tensor_copy)):
+            for u in range(2):
+                engine_copy(*dealt(w3_raw[v], w3_bf[u], 2 * u, 2 * u + 2, 2 * v, 2 * v + 2))
+        for u in range(2):
+            cols = slice(u * H // 2, (u + 1) * H // 2)
+            nc.vector.quantize_mx(out=w3_codes[:, cols].bitcast(FP8X4), scales=w3_scales[:, cols], in_=w3_bf[u][:])
+        for c in range(4):
             activate(c)
-        for c in range(2):
-            hidden(c)
-        third = linear_branch(2)
+            linear_branch(c)
         cut = PAIR + CHUNK // 2
-        nc.vector.tensor_tensor(h_of(PAIR, cut), third[:, 0 : CHUNK // 2], act[1][:, 0 : CHUNK // 2], MULT)
+        for j0, j1 in ((0, CHUNK), (CHUNK, PAIR), (PAIR, cut)):
+            hidden(j0, j1)
         quantise_hidden(0, PAIR)
-        first_bank = psum_a.tile([P, PAIR], F32, name="first_bank", tag="ring")
+        first_bank = psum.tile([P, PAIR], F32, name="first_bank", tag="bank3")
         second_product(first_bank[:], 0, 0, PAIR)
-        nc.vector.tensor_tensor(h_of(cut, 3 * CHUNK), third[:, CHUNK // 2 : CHUNK], act[1][:, CHUNK // 2 : CHUNK], MULT)
-        hidden(3)
+        for j0, j1 in ((cut, 3 * CHUNK), (3 * CHUNK, half)):
+            hidden(j0, j1)
         first = weigh("first", first_bank[:], 0, PAIR)
-        quantise_hidden(PAIR, S // 2)
-        for c in (4, 5):
-            copy_aside(c)
-        for c in (6, 7):
-            activate(c)
-        for c in (6, 7):
-            copy_aside(c)
-        for u in (2, 3):
-            nc.gpsimd.tensor_tensor(h_of(u * PAIR, (u + 1) * PAIR), lin[u][:], act[u][:], MULT)
+        quantise_hidden(PAIR, half)
         nc.vector.tensor_copy(places(0, 0, PAIR), first[:])
-        both_bank = psum_a.tile([P, 2, PAIR], F32, name="both_bank", tag="ring")
+        for c in range(4, 8):
+            linear_branch(c)
+            copy_aside(max(c * CHUNK, half + HELP), (c + 1) * CHUNK)
+            activate(c)
+        hidden(half, half + HELP)
+        hidden_aside(half + HELP, half + PAIR)
+        hidden_aside(half + PAIR, S)
+        both_bank = psum.tile([P, 2, PAIR], F32, name="both_bank", tag="bank4")
         second_product(both_bank[:, 0, :], 1, 0, PAIR)
-        second_product(both_bank[:, 1, :], 0, PAIR, S // 2)
-        held_bank = psum_a.tile([P, PAIR], F32, name="held_bank", tag="ring")
-        second_product(held_bank[:], 1, PAIR, S // 2)
+        second_product(both_bank[:, 1, :], 0, PAIR, half)
+        held_bank = psum.tile([P, PAIR], F32, name="held_bank", tag="bank5")
+        second_product(held_bank[:], 1, PAIR, half)
         second = weigh("second", both_bank[:, 0, :], 0, PAIR)
-        third_y = weigh("third_y", both_bank[:, 1, :], PAIR, S // 2)
+        third = weigh("third", both_bank[:, 1, :], PAIR, half)
         nc.vector.tensor_copy(places(1, 0, PAIR), second[:])
-        nc.vector.tensor_copy(places(0, PAIR, S // 2), third_y[:])
-        quantise_hidden(S // 2, S)
-        held = keep.tile([P, PAIR], F32, name="held", tag="lin3", align_bytes=64)
+        nc.vector.tensor_copy(places(0, PAIR, half), third[:])
+        quantise_hidden(half, S)
+        held = keep.tile([P, PAIR], F32, name="held", tag="lin", align_bytes=64)
         nc.scalar.copy(held[:], held_bank[:])
-        nc.vector.tensor_tensor(places(1, PAIR, S // 2), held[:], gate_row[:, PAIR : S // 2], MULT)
+        nc.vector.tensor_tensor(places(1, PAIR, half), held[:], gate_row[:, PAIR:half], MULT)
         for m in range(2):
-            bank = psum_b.tile([P, S // 2], F32, name="bank_b")
-            second_product(bank[:], m, S // 2, S)
-            last = keep.tile([P, S // 2], F32, name=f"last{m}")
-            nc.scalar.copy(last[:], bank[:])
-            nc.vector.tensor_tensor(places(m, S // 2, S), last[:], gate_row[:, S // 2 : S], MULT)
+            last = keep.tile([P, half], F32, name=f"last{m}")
+            for j0 in (half, half + PAIR):
+                bank = psum.tile([P, PAIR], F32, name=f"last_bank{m}_{j0}", tag=f"bank{2 * m + (j0 - half) // PAIR}")
+                second_product(bank[:], m, j0, j0 + PAIR)
+                nc.scalar.copy(last[:, j0 - half : j0 - half + PAIR], bank[:])
+            nc.vector.tensor_tensor(places(m, half, S), last[:], gate_row[:, half:S], MULT)
         nc.sync.dma_start(out[0:P, :], windows[0][:])
         nc.sync.dma_start(out[P : 2 * P, 0 : U // 2], windows[1][:, 0 : U // 2])
         nc.scalar.dma_start(out[P : 2 * P, U // 2 : U], windows[1][:, U // 2 : U])

@@ -21,7 +21,7 @@ PACK = 4
 CHUNK = 128
 PAIR = 2 * CHUNK
 GATHER = 512
-HELP = 64
+EARLY = 48
 
 
 def tile_picked_route2_glusilu_p_kernel(tc, x_words, x_scales, gate, w1, w3, w2_words, w2_scales, offs, dst, out):
@@ -35,7 +35,7 @@ def tile_picked_route2_glusilu_p_kernel(tc, x_words, x_scales, gate, w1, w3, w2_
         dst_sb = keep.tile([P, S // 16], U16, name="dst_sb")
         xs = reuse.tile([P, T], U8, name="xs", offset=2 * T, align_bytes=64)
         w1_raw = reuse.tile([P, PACK, H], F32, name="w1_raw", offset=9 * T, align_bytes=64)
-        seed = reuse.tile([P, 32], F32, name="seed", offset=9 * T // 2, align_bytes=64)
+        seed = reuse.tile([P, 32], F32, name="seed", offset=9 * T // 2 - 64, align_bytes=64)
         zeros = keep.tile([P, 32], F32, name="zeros")
         x_planes = keep.tile([P, S], U8, name="x_planes", align_bytes=64)
         window1 = keep.tile([P, U], F32, name="window1")
@@ -52,6 +52,12 @@ def tile_picked_route2_glusilu_p_kernel(tc, x_words, x_scales, gate, w1, w3, w2_
         nc.sync.dma_start(w1_raw[:, 2:4, :], w1_rows[:, 2:4, :])
         xw = reuse.tile([P, T], U32, name="xw", offset=9 * T // 2, align_bytes=64)
         nc.sync.dma_start(xw[:].bitcast(I32), x_words[0].rearrange("p n t -> p (n t)").bitcast(I32))
+        w3_rows = w3.rearrange("(p j) c -> p j c", j=PACK)
+        w3_raw = [
+            reuse.tile([P, 2, H], F32, name="w3_raw0", offset=7 * T // 2, align_bytes=64),
+            reuse.tile([P, 2, H], F32, name="w3_raw1", offset=9 * T, align_bytes=64),
+        ]
+        nc.sync.dma_start(w3_raw[0][:], w3_rows[:, 0:2, :])
         nc.scalar.activation(window1[:], zeros[:, 0:1].to_broadcast([P, U]), SILU)
         nc.vector.memset(x_planes[:].bitcast(I32), 0)
 
@@ -73,50 +79,45 @@ def tile_picked_route2_glusilu_p_kernel(tc, x_words, x_scales, gate, w1, w3, w2_
         nc.vector.tensor_copy(picked_s[:], xs[:].indirect(offs_sb[:]))
         for r in range(4):
             nc.sync.dma_start(
-                x_planes[32 * r : 32 * r + 4, :].bitcast(I32), picked_s[32 + 16 * r : 48 + 16 * r : 4, :].bitcast(I32)
+                x_planes[r:P:32, :].bitcast(I32), picked_s[32 + 4 * r : 96 : 16, :].bitcast(I32)
             )
-        w3_rows = w3.rearrange("(p j) c -> p j c", j=PACK)
-        w3_raw = [
-            reuse.tile([P, 2, H], F32, name="w3_raw0", offset=3 * T // 2, align_bytes=64),
-            reuse.tile([P, 2, H], F32, name="w3_raw1", offset=9 * T, align_bytes=64),
-        ]
-        for v in range(2):
-            nc.sync.dma_start(w3_raw[v][:], w3_rows[:, 2 * v : 2 * v + 2, :])
-        window0 = reuse.tile([P, U], F32, name="window0", offset=5 * T // 2, align_bytes=64)
+        nc.sync.dma_start(w3_raw[1][:], w3_rows[:, 2:4, :])
+        window0 = reuse.tile([P, U], F32, name="window0", offset=T // 2, align_bytes=64)
         nc.vector.memset(window0[:], 0.0)
         windows = [window0, window1]
         w2w = reuse.tile([P, 2 * N], U8, name="w2w", offset=10 * T, align_bytes=64)
         nc.sync.dma_start(w2w[:].bitcast(I32), w2_words[0].bitcast(I32))
         w1_scales = keep.tile([P, H], U8, name="w1_scales", align_bytes=64)
         nc.vector.quantize_mx(out=w1_codes[:].bitcast(FP8X4), scales=w1_scales[:], in_=w1_bf[:])
-        w2s = keep.tile([P, N], U8, name="w2s", tag="w1_bf", align_bytes=64)
-        nc.vector.memset(w2s[:].bitcast(I32), 0)
+        w2s = keep.tile([P, N], U8, name="w2s", align_bytes=64)
+        nc.gpsimd.memset(w2s[:].bitcast(I32), 0)
         for r in range(4):
-            nc.sync.dma_start(w2s[r:P:32, :].bitcast(I32), w2_scales[0, r:16:4, :].bitcast(I32))
+            nc.gpsimd.dma_start(w2s[r:P:32, :].bitcast(I32), w2_scales[0, r:16:4, :].bitcast(I32))
         for g in range(S // GATHER):
             cols = slice(g * GATHER // 16, (g + 1) * GATHER // 16)
             nc.vector.tensor_copy(picked_w[g][:], xw[:].indirect(offs_sb[:, cols]))
         gate_row = reuse.tile([P, S], F32, name="gate_row", offset=9 * T // 2, align_bytes=64)
         nc.sync.dma_start(gate_row[:], gate)
 
-        def first_product(bank, codes, scales, c):
-            g, at = divmod(c * CHUNK, GATHER)
+        def first_product(bank, codes, scales, j0, j1):
+            g, at = divmod(j0, GATHER)
             for t in range(PACK):
                 nc.tensor.matmul_mx(
                     out=bank[:, t, :],
                     lhsT=codes[:, t * P : (t + 1) * P].bitcast(FP8X4),
                     lhsT_scale=scales[:, t * P : (t + 1) * P],
-                    rhs=picked_w[g][:, at : at + CHUNK].bitcast(FP8X4),
-                    rhs_scale=x_planes[:, c * CHUNK : (c + 1) * CHUNK],
+                    rhs=picked_w[g][:, at : at + j1 - j0].bitcast(FP8X4),
+                    rhs_scale=x_planes[:, j0:j1],
                     start=True,
                     stop=True,
                 )
 
         half = S // 2
-        h_bf = keep.tile([P, (S - CHUNK) * PACK], BF16, name="h_bf", align_bytes=64)
+        BACK = PAIR + EARLY
+        h_bf = keep.tile([P, (S - BACK) * PACK], BF16, name="h_bf", align_bytes=64)
         h_codes = keep.tile([P, S], U32, name="h_codes", align_bytes=64)
         h_scales = keep.tile([P, S], U8, name="h_scales", align_bytes=64)
-        act_early = reuse.tile([P, half, PACK], F32, name="act_early", offset=T // 2, align_bytes=64)
+        act_early = keep.tile([P, half, PACK], F32, name="act_early", align_bytes=64)
         act_late = keep.tile([P, half, PACK], F32, name="act_late", align_bytes=64)
         lin = keep.tile([P, half, PACK], F32, name="lin", tag="lin", align_bytes=64)
 
@@ -124,27 +125,30 @@ def tile_picked_route2_glusilu_p_kernel(tc, x_words, x_scales, gate, w1, w3, w2_
             return act_early[:, j0:j1, :] if j0 < half else act_late[:, j0 - half : j1 - half, :]
 
         def h_columns(j0, j1):
-            back = CHUNK if j0 >= half else 0
+            back = BACK if j0 >= half else 0
             return h_bf[:, (j0 - back) * PACK : (j1 - back) * PACK]
 
         def h_of(j0, j1):
             return h_columns(j0, j1).rearrange("p (n t) -> p n t", t=PACK)
 
-        def activate(c):
-            bank = psum.tile([P, PACK, CHUNK], F32, name=f"gate_bank{c}", tag=f"bank{c}")
-            first_product(bank, w1_codes, w1_scales, c)
+        def gate_branch(c):
+            bank = psum.tile([P, PACK, CHUNK], F32, name=f"gate_bank{c}", tag=f"bank{(0, 1, 2, 3, 0, 2, 3, 2)[c]}")
+            first_product(bank, w1_codes, w1_scales, c * CHUNK, (c + 1) * CHUNK)
+            return bank
+
+        def activate(c, bank):
             nc.scalar.activation(act(c * CHUNK, (c + 1) * CHUNK), bank[:].rearrange("p t n -> p n t"), SILU)
 
         linear = {}
 
-        def linear_branch(c):
-            bank = psum.tile([P, PACK, CHUNK], F32, name=f"linear_bank{c}", tag=f"bank{(c + 4) % 8}")
-            first_product(bank, w3_codes, w3_scales, c)
-            linear[c] = bank[:].rearrange("p t n -> p n t")
+        def linear_branch(j0, j1, tag):
+            bank = psum.tile([P, PACK, j1 - j0], F32, name=f"linear_bank{j0}", tag=tag)
+            first_product(bank, w3_codes, w3_scales, j0, j1)
+            linear[j0] = bank[:].rearrange("p t n -> p n t")
 
         def in_bank(j0, j1):
-            c = j0 // CHUNK
-            return linear[c][:, j0 - c * CHUNK : j1 - c * CHUNK]
+            start = max(j for j in linear if j <= j0)
+            return linear[start][:, j0 - start : j1 - start]
 
         def hidden(j0, j1):
             nc.vector.tensor_tensor(h_of(j0, j1), in_bank(j0, j1), act(j0, j1), MULT)
@@ -185,31 +189,42 @@ def tile_picked_route2_glusilu_p_kernel(tc, x_words, x_scales, gate, w1, w3, w2_
         for u in range(2):
             cols = slice(u * H // 2, (u + 1) * H // 2)
             nc.vector.quantize_mx(out=w3_codes[:, cols].bitcast(FP8X4), scales=w3_scales[:, cols], in_=w3_bf[u][:])
-        for c in range(4):
-            activate(c)
-            linear_branch(c)
+        for c in range(3):
+            activate(c, gate_branch(c))
+        bank3 = gate_branch(3)
+        activate(4, gate_branch(4))
+        narrow = CHUNK // 2
+        linear_branch(0, CHUNK, "bank4")
+        linear_branch(CHUNK, PAIR, "bank5")
+        linear_branch(half, half + narrow, "bank1")
+        linear_branch(PAIR, 3 * CHUNK, "bank6")
+        linear_branch(3 * CHUNK, half, "bank7")
+        copy_aside(half, half + narrow)
+        activate(3, bank3)
         cut = PAIR + CHUNK // 2
         for j0, j1 in ((0, CHUNK), (CHUNK, PAIR), (PAIR, cut)):
             hidden(j0, j1)
         quantise_hidden(0, PAIR)
-        first_bank = psum.tile([P, PAIR], F32, name="first_bank", tag="bank3")
+        hidden_aside(half, half + EARLY)
+        first_bank = psum.tile([P, PAIR], F32, name="first_bank", tag="bank4")
         second_product(first_bank[:], 0, 0, PAIR)
         for j0, j1 in ((cut, 3 * CHUNK), (3 * CHUNK, half)):
             hidden(j0, j1)
         first = weigh("first", first_bank[:], 0, PAIR)
         quantise_hidden(PAIR, half)
         nc.vector.tensor_copy(places(0, 0, PAIR), first[:])
-        for c in range(4, 8):
-            linear_branch(c)
-            copy_aside(max(c * CHUNK, half + HELP), (c + 1) * CHUNK)
-            activate(c)
-        hidden(half, half + HELP)
-        hidden_aside(half + HELP, half + PAIR)
+        linear_branch(half + narrow, half + CHUNK, "bank0")
+        copy_aside(half + narrow, half + CHUNK)
+        for c, tag in ((5, "bank5"), (6, "bank1"), (7, "bank6")):
+            activate(c, gate_branch(c))
+            linear_branch(c * CHUNK, (c + 1) * CHUNK, tag)
+            copy_aside(c * CHUNK, (c + 1) * CHUNK)
+        hidden_aside(half + EARLY, half + PAIR)
         hidden_aside(half + PAIR, S)
-        both_bank = psum.tile([P, 2, PAIR], F32, name="both_bank", tag="bank4")
+        both_bank = psum.tile([P, 2, PAIR], F32, name="both_bank", tag="bank7")
         second_product(both_bank[:, 0, :], 1, 0, PAIR)
         second_product(both_bank[:, 1, :], 0, PAIR, half)
-        held_bank = psum.tile([P, PAIR], F32, name="held_bank", tag="bank5")
+        held_bank = psum.tile([P, PAIR], F32, name="held_bank", tag="bank4")
         second_product(held_bank[:], 1, PAIR, half)
         second = weigh("second", both_bank[:, 0, :], 0, PAIR)
         third = weigh("third", both_bank[:, 1, :], PAIR, half)

@@ -90,7 +90,7 @@ def tile_picked_route2_glusilu_p_kernel(tc, x_words, x_scales, gate, w1, w3, w2_
         w1_scales = keep.tile([P, H], U8, name="w1_scales", align_bytes=64)
         nc.vector.quantize_mx(out=w1_codes[:].bitcast(FP8X4), scales=w1_scales[:], in_=w1_bf[:])
         w2s = keep.tile([P, N], U8, name="w2s", align_bytes=64)
-        nc.gpsimd.memset(w2s[:].bitcast(I32), 0)
+        nc.vector.memset(w2s[:].bitcast(I32), 0)
         for r in range(4):
             nc.gpsimd.dma_start(w2s[r:P:32, :].bitcast(I32), w2_scales[0, r:16:4, :].bitcast(I32))
         for g in range(S // GATHER):

@@ -55,7 +55,7 @@ def tile_picked_route2_glusilu_p_kernel(tc, x_words, x_scales, gate, w1, w3, w2_
         w3_rows = w3.rearrange("(p j) c -> p j c", j=PACK)
         w3_raw = [
             reuse.tile([P, 2, H], F32, name="w3_raw0", offset=7 * T // 2, align_bytes=64),
-            reuse.tile([P, 2, H], F32, name="w3_raw1", offset=9 * T, align_bytes=64),
+            reuse.tile([P, 2, H], F32, name="w3_raw1", offset=5 * T // 2, align_bytes=64),
         ]
         nc.sync.dma_start(w3_raw[0][:], w3_rows[:, 0:2, :])
         nc.scalar.activation(window1[:], zeros[:, 0:1].to_broadcast([P, U]), SILU)
@@ -136,8 +136,8 @@ def tile_picked_route2_glusilu_p_kernel(tc, x_words, x_scales, gate, w1, w3, w2_
             first_product(bank, w1_codes, w1_scales, c * CHUNK, (c + 1) * CHUNK)
             return bank
 
-        def activate(c, bank):
-            nc.scalar.activation(act(c * CHUNK, (c + 1) * CHUNK), bank[:].rearrange("p t n -> p n t"), SILU)
+        def activate(c, bank, n0=0, n1=CHUNK):
+            nc.scalar.activation(act(c * CHUNK + n0, c * CHUNK + n1), bank[:].rearrange("p t n -> p n t")[:, n0:n1], SILU)
 
         linear = {}
 
@@ -192,7 +192,8 @@ def tile_picked_route2_glusilu_p_kernel(tc, x_words, x_scales, gate, w1, w3, w2_
         for c in range(3):
             activate(c, gate_branch(c))
         bank3 = gate_branch(3)
-        activate(4, gate_branch(4))
+        bank4 = gate_branch(4)
+        activate(4, bank4, 0, CHUNK // 2)
         narrow = CHUNK // 2
         linear_branch(0, CHUNK, "bank4")
         linear_branch(CHUNK, PAIR, "bank5")
@@ -213,6 +214,7 @@ def tile_picked_route2_glusilu_p_kernel(tc, x_words, x_scales, gate, w1, w3, w2_
         first = weigh("first", first_bank[:], 0, PAIR)
         quantise_hidden(PAIR, half)
         nc.vector.tensor_copy(places(0, 0, PAIR), first[:])
+        activate(4, bank4, narrow, CHUNK)
         linear_branch(half + narrow, half + CHUNK, "bank0")
         copy_aside(half + narrow, half + CHUNK)
         for c, tag in ((5, "bank5"), (6, "bank1"), (7, "bank6")):

@@ -41,24 +41,25 @@ def tile_picked_route2_glusilu_p_kernel(tc, x_words, x_scales, gate, w1, w3, w2_
         window1 = keep.tile([P, U], F32, name="window1")
 
         w1_rows = w1.rearrange("(p j) c -> p j c", j=PACK)
-        nc.sync.dma_start(w1_raw[:, 0:2, :], w1_rows[:, 0:2, :])
+        nc.sync.dma_start(w1_raw[:], w1_rows)
         nc.sync.dma_start(offs_sb[:], offs)
         nc.sync.dma_start(dst_sb[:], dst)
         nc.vector.memset(seed[:], 0.0)
-        nc.vector.memset(w1_raw[:, 2, 0:32], 0.0)
         nc.vector.memset(xs[:].bitcast(I32), 0)
-        nc.vector.tensor_tensor(zeros[:], seed[:], w1_raw[:, 2, 0:32], MULT)
+        nc.vector.tensor_copy(zeros[:], seed[:])
         nc.sync.dma_start(xs[32:96:4, :].bitcast(I32), x_scales[0].bitcast(I32))
-        nc.sync.dma_start(w1_raw[:, 2:4, :], w1_rows[:, 2:4, :])
         xw = reuse.tile([P, T], U32, name="xw", offset=9 * T // 2, align_bytes=64)
         nc.sync.dma_start(xw[:].bitcast(I32), x_words[0].rearrange("p n t -> p (n t)").bitcast(I32))
         w3_rows = w3.rearrange("(p j) c -> p j c", j=PACK)
-        w3_raw = [
-            reuse.tile([P, 2, H], F32, name="w3_raw0", offset=7 * T // 2, align_bytes=64),
-            reuse.tile([P, 2, H], F32, name="w3_raw1", offset=5 * T // 2, align_bytes=64),
-        ]
-        nc.sync.dma_start(w3_raw[0][:], w3_rows[:, 0:2, :])
-        nc.scalar.activation(window1[:], zeros[:, 0:1].to_broadcast([P, U]), SILU)
+        w3_upper = reuse.tile([P, 2, H], F32, name="w3_upper", offset=7 * T // 2, align_bytes=64)
+        nc.sync.dma_start(w3_upper[:], w3_rows[:, 0:2, :])
+
+        def clear(window):
+            nc.scalar.activation(
+                window[:].rearrange("p (r c) -> p r c", c=32), zeros[:].unsqueeze(1).to_broadcast([P, U // 32, 32]), SILU
+            )
+
+        clear(window1)
         nc.vector.memset(x_planes[:].bitcast(I32), 0)
 
         def dealt(raw, grouped, t0, t1, j0, j1):
@@ -81,12 +82,16 @@ def tile_picked_route2_glusilu_p_kernel(tc, x_words, x_scales, gate, w1, w3, w2_
             nc.sync.dma_start(
                 x_planes[r:P:32, :].bitcast(I32), picked_s[32 + 4 * r : 96 : 16, :].bitcast(I32)
             )
-        nc.sync.dma_start(w3_raw[1][:], w3_rows[:, 2:4, :])
-        window0 = reuse.tile([P, U], F32, name="window0", offset=T // 2, align_bytes=64)
-        nc.vector.memset(window0[:], 0.0)
+        w2w_at = 2 * T + 64
+        w3_lower = reuse.tile([P, 2, H], F32, name="w3_lower", offset=w2w_at + 2 * N, align_bytes=64)
+        nc.sync.dma_start(w3_lower[:], w3_rows[:, 2:4, :])
+        window0 = reuse.tile([P, U], F32, name="window0", offset=9 * T, align_bytes=64)
+        clear(window0)
         windows = [window0, window1]
-        w2w = reuse.tile([P, 2 * N], U8, name="w2w", offset=10 * T, align_bytes=64)
+        w2w = reuse.tile([P, 2 * N], U8, name="w2w", offset=w2w_at, align_bytes=64)
         nc.sync.dma_start(w2w[:].bitcast(I32), w2_words[0].bitcast(I32))
+        gate_row = reuse.tile([P, S], F32, name="gate_row", offset=w2w_at - 4 * S, align_bytes=64)
+        nc.sync.dma_start(gate_row[:], gate)
         w1_scales = keep.tile([P, H], U8, name="w1_scales", align_bytes=64)
         nc.vector.quantize_mx(out=w1_codes[:].bitcast(FP8X4), scales=w1_scales[:], in_=w1_bf[:])
         w2s = keep.tile([P, N], U8, name="w2s", align_bytes=64)
@@ -96,8 +101,6 @@ def tile_picked_route2_glusilu_p_kernel(tc, x_words, x_scales, gate, w1, w3, w2_
         for g in range(S // GATHER):
             cols = slice(g * GATHER // 16, (g + 1) * GATHER // 16)
             nc.vector.tensor_copy(picked_w[g][:], xw[:].indirect(offs_sb[:, cols]))
-        gate_row = reuse.tile([P, S], F32, name="gate_row", offset=9 * T // 2, align_bytes=64)
-        nc.sync.dma_start(gate_row[:], gate)
 
         def first_product(bank, codes, scales, j0, j1):
             g, at = divmod(j0, GATHER)
@@ -131,20 +134,27 @@ def tile_picked_route2_glusilu_p_kernel(tc, x_words, x_scales, gate, w1, w3, w2_
         def h_of(j0, j1):
             return h_columns(j0, j1).rearrange("p (n t) -> p n t", t=PACK)
 
-        def gate_branch(c):
-            bank = psum.tile([P, PACK, CHUNK], F32, name=f"gate_bank{c}", tag=f"bank{(0, 1, 2, 3, 0, 2, 3, 2)[c]}")
-            first_product(bank, w1_codes, w1_scales, c * CHUNK, (c + 1) * CHUNK)
-            return bank
+        gated, linear = {}, {}
 
-        def activate(c, bank, n0=0, n1=CHUNK):
-            nc.scalar.activation(act(c * CHUNK + n0, c * CHUNK + n1), bank[:].rearrange("p t n -> p n t")[:, n0:n1], SILU)
+        def branch(banks, codes, scales, j0, j1, bank):
+            first_product(bank, codes, scales, j0, j1)
+            banks[j0] = bank.rearrange("p t n -> p n t")
 
-        linear = {}
+        def gate_branch(c, tag):
+            bank = psum.tile([P, PACK, CHUNK], F32, name=f"gate_bank{c}", tag=tag)
+            branch(gated, w1_codes, w1_scales, c * CHUNK, (c + 1) * CHUNK, bank[:])
 
-        def linear_branch(j0, j1, tag):
-            bank = psum.tile([P, PACK, j1 - j0], F32, name=f"linear_bank{j0}", tag=tag)
-            first_product(bank, w3_codes, w3_scales, j0, j1)
-            linear[j0] = bank[:].rearrange("p t n -> p n t")
+        def linear_branch(c, tag):
+            bank = psum.tile([P, PACK, CHUNK], F32, name=f"linear_bank{c}", tag=tag)
+            branch(linear, w3_codes, w3_scales, c * CHUNK, (c + 1) * CHUNK, bank[:])
+
+        def both_branches(j0, j1, tag):
+            bank = psum.tile([P, 2, PACK, j1 - j0], F32, name=f"both_bank{j0}", tag=tag)
+            branch(linear, w3_codes, w3_scales, j0, j1, bank[:, 0])
+            branch(gated, w1_codes, w1_scales, j0, j1, bank[:, 1])
+
+        def activate(j0, j1):
+            nc.scalar.activation(act(j0, j1), gated[j0], SILU)
 
         def in_bank(j0, j1):
             start = max(j for j in linear if j <= j0)
@@ -183,50 +193,55 @@ def tile_picked_route2_glusilu_p_kernel(tc, x_words, x_scales, gate, w1, w3, w2_
             nc.vector.tensor_tensor(weighed[:], bank, gate_row[:, j0:j1], MULT)
             return weighed
 
-        for v, engine_copy in enumerate((nc.scalar.copy, nc.vector.tensor_copy)):
+        for v, (raw, engine_copy) in enumerate(((w3_upper, nc.scalar.copy), (w3_lower, nc.vector.tensor_copy))):
             for u in range(2):
-                engine_copy(*dealt(w3_raw[v], w3_bf[u], 2 * u, 2 * u + 2, 2 * v, 2 * v + 2))
-        for u in range(2):
-            cols = slice(u * H // 2, (u + 1) * H // 2)
-            nc.vector.quantize_mx(out=w3_codes[:, cols].bitcast(FP8X4), scales=w3_scales[:, cols], in_=w3_bf[u][:])
-        for c in range(3):
-            activate(c, gate_branch(c))
-        bank3 = gate_branch(3)
-        bank4 = gate_branch(4)
-        activate(4, bank4, 0, CHUNK // 2)
+                engine_copy(*dealt(raw, w3_bf[u], 2 * u, 2 * u + 2, 2 * v, 2 * v + 2))
+        for t0, t1 in ((0, 2), (2, 3), (3, 4)):
+            cols = slice(t0 * P, t1 * P)
+            u, at = divmod(t0, 2)
+            nc.vector.quantize_mx(
+                out=w3_codes[:, cols].bitcast(FP8X4),
+                scales=w3_scales[:, cols],
+                in_=w3_bf[u][:, at * P * PACK : (at + t1 - t0) * P * PACK],
+            )
         narrow = CHUNK // 2
-        linear_branch(0, CHUNK, "bank4")
-        linear_branch(CHUNK, PAIR, "bank5")
-        linear_branch(half, half + narrow, "bank1")
-        linear_branch(PAIR, 3 * CHUNK, "bank6")
-        linear_branch(3 * CHUNK, half, "bank7")
+        for c in range(4):
+            gate_branch(c, f"bank{c}")
+            activate(c * CHUNK, (c + 1) * CHUNK)
+        linear_branch(0, "bank4")
+        linear_branch(1, "bank5")
+        linear_branch(2, "bank6")
+        both_branches(half, half + narrow, "bank1")
+        linear_branch(3, "bank7")
         copy_aside(half, half + narrow)
-        activate(3, bank3)
+        activate(half, half + narrow)
         cut = PAIR + CHUNK // 2
         for j0, j1 in ((0, CHUNK), (CHUNK, PAIR), (PAIR, cut)):
             hidden(j0, j1)
         quantise_hidden(0, PAIR)
         hidden_aside(half, half + EARLY)
-        first_bank = psum.tile([P, PAIR], F32, name="first_bank", tag="bank4")
+        first_bank = psum.tile([P, PAIR], F32, name="first_bank", tag="bank3")
         second_product(first_bank[:], 0, 0, PAIR)
         for j0, j1 in ((cut, 3 * CHUNK), (3 * CHUNK, half)):
             hidden(j0, j1)
         first = weigh("first", first_bank[:], 0, PAIR)
         quantise_hidden(PAIR, half)
         nc.vector.tensor_copy(places(0, 0, PAIR), first[:])
-        activate(4, bank4, narrow, CHUNK)
-        linear_branch(half + narrow, half + CHUNK, "bank0")
+        both_branches(half + narrow, half + CHUNK, "bank2")
         copy_aside(half + narrow, half + CHUNK)
-        for c, tag in ((5, "bank5"), (6, "bank1"), (7, "bank6")):
-            activate(c, gate_branch(c))
-            linear_branch(c * CHUNK, (c + 1) * CHUNK, tag)
+        activate(half + narrow, half + CHUNK)
+        for c, gate_tag, linear_tag in ((5, "bank6", "bank0"), (6, "bank7", "bank3"), (7, "bank6", "bank7")):
+            linear_branch(c, linear_tag)
             copy_aside(c * CHUNK, (c + 1) * CHUNK)
-        hidden_aside(half + EARLY, half + PAIR)
-        hidden_aside(half + PAIR, S)
-        both_bank = psum.tile([P, 2, PAIR], F32, name="both_bank", tag="bank7")
+            gate_branch(c, gate_tag)
+            activate(c * CHUNK, (c + 1) * CHUNK)
+        hidden_aside(half + EARLY, half + CHUNK)
+        for j0 in range(half + CHUNK, S, CHUNK):
+            hidden_aside(j0, j0 + CHUNK)
+        both_bank = psum.tile([P, 2, PAIR], F32, name="both_bank", tag="bank4")
         second_product(both_bank[:, 0, :], 1, 0, PAIR)
         second_product(both_bank[:, 1, :], 0, PAIR, half)
-        held_bank = psum.tile([P, PAIR], F32, name="held_bank", tag="bank4")
+        held_bank = psum.tile([P, PAIR], F32, name="held_bank", tag="bank5")
         second_product(held_bank[:], 1, PAIR, half)
         second = weigh("second", both_bank[:, 0, :], 0, PAIR)
         third = weigh("third", both_bank[:, 1, :], PAIR, half)
@@ -239,7 +254,7 @@ def tile_picked_route2_glusilu_p_kernel(tc, x_words, x_scales, gate, w1, w3, w2_
         for m in range(2):
             last = keep.tile([P, half], F32, name=f"last{m}")
             for j0 in (half, half + PAIR):
-                bank = psum.tile([P, PAIR], F32, name=f"last_bank{m}_{j0}", tag=f"bank{2 * m + (j0 - half) // PAIR}")
+                bank = psum.tile([P, PAIR], F32, name=f"last_bank{m}_{j0}", tag=f"bank{(0, 1, 2, 3)[2 * m + (j0 - half) // PAIR]}")
                 second_product(bank[:], m, j0, j0 + PAIR)
                 nc.scalar.copy(last[:, j0 - half : j0 - half + PAIR], bank[:])
             nc.vector.tensor_tensor(places(m, half, S), last[:], gate_row[:, half:S], MULT)

@@ -15,13 +15,14 @@ FP8X4 = mybir.dt.float8_e4m3fn_x4
 FP4X4 = mybir.dt.float4_e2m1fn_x4
 MULT = mybir.AluOpType.mult
 SILU = mybir.ActivationFunctionType.Silu
+COPY = mybir.ActivationFunctionType.Copy
 
 P = 128
 PACK = 4
 CHUNK = 128
 PAIR = 2 * CHUNK
 GATHER = 512
-EARLY = 48
+CUT = 448
 
 
 def tile_picked_route2_glusilu_p_kernel(tc, x_words, x_scales, gate, w1, w3, w2_words, w2_scales, offs, dst, out):
@@ -115,83 +116,63 @@ def tile_picked_route2_glusilu_p_kernel(tc, x_words, x_scales, gate, w1, w3, w2_
                     stop=True,
                 )
 
-        half = S // 2
-        BACK = PAIR + EARLY
-        h_bf = keep.tile([P, (S - BACK) * PACK], BF16, name="h_bf", align_bytes=64)
+        h_bf = keep.tile([P, S * PACK], BF16, name="h_bf", align_bytes=64)
         h_codes = keep.tile([P, S], U32, name="h_codes", align_bytes=64)
         h_scales = keep.tile([P, S], U8, name="h_scales", align_bytes=64)
-        act_early = keep.tile([P, half, PACK], F32, name="act_early", align_bytes=64)
-        act_late = keep.tile([P, half, PACK], F32, name="act_late", align_bytes=64)
-        lin = keep.tile([P, half, PACK], F32, name="lin", tag="lin", align_bytes=64)
-
-        def act(j0, j1):
-            return act_early[:, j0:j1, :] if j0 < half else act_late[:, j0 - half : j1 - half, :]
-
-        def h_columns(j0, j1):
-            back = BACK if j0 >= half else 0
-            return h_bf[:, (j0 - back) * PACK : (j1 - back) * PACK]
-
-        def h_of(j0, j1):
-            return h_columns(j0, j1).rearrange("p (n t) -> p n t", t=PACK)
-
-        gated, linear = {}, {}
-
-        def branch(banks, codes, scales, j0, j1, bank):
-            first_product(bank, codes, scales, j0, j1)
-            banks[j0] = bank.rearrange("p t n -> p n t")
+        act = [keep.tile([P, CHUNK, PACK], F32, name=f"act{c}", align_bytes=64) for c in range(S // CHUNK)]
+        linear = {}
 
         def gate_branch(c, tag):
             bank = psum.tile([P, PACK, CHUNK], F32, name=f"gate_bank{c}", tag=tag)
-            branch(gated, w1_codes, w1_scales, c * CHUNK, (c + 1) * CHUNK, bank[:])
+            first_product(bank, w1_codes, w1_scales, c * CHUNK, (c + 1) * CHUNK)
+            nc.scalar.activation(act[c][:], bank[:].rearrange("p t n -> p n t"), SILU)
 
         def linear_branch(c, tag):
             bank = psum.tile([P, PACK, CHUNK], F32, name=f"linear_bank{c}", tag=tag)
-            branch(linear, w3_codes, w3_scales, c * CHUNK, (c + 1) * CHUNK, bank[:])
+            first_product(bank, w3_codes, w3_scales, c * CHUNK, (c + 1) * CHUNK)
+            linear[c] = bank
 
-        def both_branches(j0, j1, tag):
-            bank = psum.tile([P, 2, PACK, j1 - j0], F32, name=f"both_bank{j0}", tag=tag)
-            branch(linear, w3_codes, w3_scales, j0, j1, bank[:, 0])
-            branch(gated, w1_codes, w1_scales, j0, j1, bank[:, 1])
+        def hidden(c):
+            to = h_bf[:, c * CHUNK * PACK : (c + 1) * CHUNK * PACK].rearrange("p (n t) -> p n t", t=PACK)
+            nc.vector.tensor_tensor(to, linear[c][:].rearrange("p t n -> p n t"), act[c][:], MULT)
 
-        def activate(j0, j1):
-            nc.scalar.activation(act(j0, j1), gated[j0], SILU)
-
-        def in_bank(j0, j1):
-            start = max(j for j in linear if j <= j0)
-            return linear[start][:, j0 - start : j1 - start]
-
-        def hidden(j0, j1):
-            nc.vector.tensor_tensor(h_of(j0, j1), in_bank(j0, j1), act(j0, j1), MULT)
-
-        def copy_aside(j0, j1):
-            nc.scalar.copy(lin[:, j0 - half : j1 - half, :], in_bank(j0, j1))
-
-        def hidden_aside(j0, j1):
-            nc.gpsimd.tensor_tensor(h_of(j0, j1), lin[:, j0 - half : j1 - half, :], act(j0, j1), MULT)
-
-        def quantise_hidden(j0, j1):
-            nc.vector.quantize_mx(
-                out=h_codes[:, j0:j1].bitcast(FP8X4), scales=h_scales[:, j0:j1], in_=h_columns(j0, j1)
-            )
-
-        def second_product(into, m, j0, j1):
+        def second_product(q, m, tag):
+            bank = psum.tile([P, PAIR], F32, name=f"y_bank{m}_{q}", tag=tag)
+            cols = slice(q * PAIR, (q + 1) * PAIR)
             nc.tensor.matmul_mx(
-                out=into,
+                out=bank[:],
                 lhsT=w2w[:, 2 * m * P : 2 * (m + 1) * P].bitcast(FP4X4),
                 lhsT_scale=w2s[:, m * P : (m + 1) * P],
-                rhs=h_codes[:, j0:j1].bitcast(FP8X4),
-                rhs_scale=h_scales[:, j0:j1],
+                rhs=h_codes[:, cols].bitcast(FP8X4),
+                rhs_scale=h_scales[:, cols],
                 start=True,
                 stop=True,
             )
+            return bank
+
+        y_upper = keep.tile([P, S], F32, name="y_upper")
+        lower_banks = {}
+
+        def quantise_hidden(q, lower_tag, upper_tag):
+            cols = slice(q * PAIR, (q + 1) * PAIR)
+            nc.vector.quantize_mx(
+                out=h_codes[:, cols].bitcast(FP8X4),
+                scales=h_scales[:, cols],
+                in_=h_bf[:, q * PAIR * PACK : (q + 1) * PAIR * PACK],
+            )
+            lower_banks[q] = second_product(q, 1, lower_tag)
+            nc.scalar.copy(y_upper[:, cols], second_product(q, 0, upper_tag)[:])
 
         def places(m, j0, j1):
             return windows[m][:].indirect(dst_sb[:, j0 // 16 : j1 // 16])
 
-        def weigh(name, bank, j0, j1):
-            weighed = keep.tile([P, j1 - j0], F32, name=name)
-            nc.vector.tensor_tensor(weighed[:], bank, gate_row[:, j0:j1], MULT)
-            return weighed
+        def put_lower(q):
+            weighed = keep.tile([P, PAIR], F32, name=f"weighed{q}")
+            nc.vector.tensor_tensor(weighed[:], lower_banks[q][:], gate_row[:, q * PAIR : (q + 1) * PAIR], MULT)
+            nc.scalar.activation(places(1, q * PAIR, (q + 1) * PAIR), weighed[:], COPY)
+
+        def put_upper(j0, j1):
+            nc.vector.tensor_tensor(places(0, j0, j1), y_upper[:, j0:j1], gate_row[:, j0:j1], MULT)
 
         for v, (raw, engine_copy) in enumerate(((w3_upper, nc.scalar.copy), (w3_lower, nc.vector.tensor_copy))):
             for u in range(2):
@@ -204,60 +185,34 @@ def tile_picked_route2_glusilu_p_kernel(tc, x_words, x_scales, gate, w1, w3, w2_
                 scales=w3_scales[:, cols],
                 in_=w3_bf[u][:, at * P * PACK : (at + t1 - t0) * P * PACK],
             )
-        narrow = CHUNK // 2
-        for c in range(4):
-            gate_branch(c, f"bank{c}")
-            activate(c * CHUNK, (c + 1) * CHUNK)
-        linear_branch(0, "bank4")
-        linear_branch(1, "bank5")
-        linear_branch(2, "bank6")
-        both_branches(half, half + narrow, "bank1")
-        linear_branch(3, "bank7")
-        copy_aside(half, half + narrow)
-        activate(half, half + narrow)
-        cut = PAIR + CHUNK // 2
-        for j0, j1 in ((0, CHUNK), (CHUNK, PAIR), (PAIR, cut)):
-            hidden(j0, j1)
-        quantise_hidden(0, PAIR)
-        hidden_aside(half, half + EARLY)
-        first_bank = psum.tile([P, PAIR], F32, name="first_bank", tag="bank3")
-        second_product(first_bank[:], 0, 0, PAIR)
-        for j0, j1 in ((cut, 3 * CHUNK), (3 * CHUNK, half)):
-            hidden(j0, j1)
-        first = weigh("first", first_bank[:], 0, PAIR)
-        quantise_hidden(PAIR, half)
-        nc.vector.tensor_copy(places(0, 0, PAIR), first[:])
-        both_branches(half + narrow, half + CHUNK, "bank2")
-        copy_aside(half + narrow, half + CHUNK)
-        activate(half + narrow, half + CHUNK)
-        for c, gate_tag, linear_tag in ((5, "bank6", "bank0"), (6, "bank7", "bank3"), (7, "bank6", "bank7")):
-            linear_branch(c, linear_tag)
-            copy_aside(c * CHUNK, (c + 1) * CHUNK)
-            gate_branch(c, gate_tag)
-            activate(c * CHUNK, (c + 1) * CHUNK)
-        hidden_aside(half + EARLY, half + CHUNK)
-        for j0 in range(half + CHUNK, S, CHUNK):
-            hidden_aside(j0, j0 + CHUNK)
-        both_bank = psum.tile([P, 2, PAIR], F32, name="both_bank", tag="bank4")
-        second_product(both_bank[:, 0, :], 1, 0, PAIR)
-        second_product(both_bank[:, 1, :], 0, PAIR, half)
-        held_bank = psum.tile([P, PAIR], F32, name="held_bank", tag="bank5")
-        second_product(held_bank[:], 1, PAIR, half)
-        second = weigh("second", both_bank[:, 0, :], 0, PAIR)
-        third = weigh("third", both_bank[:, 1, :], PAIR, half)
-        nc.vector.tensor_copy(places(1, 0, PAIR), second[:])
-        nc.vector.tensor_copy(places(0, PAIR, half), third[:])
-        quantise_hidden(half, S)
-        held = keep.tile([P, PAIR], F32, name="held", tag="lin", align_bytes=64)
-        nc.scalar.copy(held[:], held_bank[:])
-        nc.vector.tensor_tensor(places(1, PAIR, half), held[:], gate_row[:, PAIR:half], MULT)
-        for m in range(2):
-            last = keep.tile([P, half], F32, name=f"last{m}")
-            for j0 in (half, half + PAIR):
-                bank = psum.tile([P, PAIR], F32, name=f"last_bank{m}_{j0}", tag=f"bank{(0, 1, 2, 3)[2 * m + (j0 - half) // PAIR]}")
-                second_product(bank[:], m, j0, j0 + PAIR)
-                nc.scalar.copy(last[:, j0 - half : j0 - half + PAIR], bank[:])
-            nc.vector.tensor_tensor(places(m, half, S), last[:], gate_row[:, half:S], MULT)
-        nc.sync.dma_start(out[0:P, :], windows[0][:])
-        nc.sync.dma_start(out[P : 2 * P, 0 : U // 2], windows[1][:, 0 : U // 2])
-        nc.scalar.dma_start(out[P : 2 * P, U // 2 : U], windows[1][:, U // 2 : U])
+        pairs = (0, 1, 2, 3)
+        chunks = [2 * q + e for q in pairs for e in range(2)]
+        for n in range(4):
+            gate_branch(chunks[n], f"bank{n}")
+        linear_branch(chunks[0], "bank4")
+        linear_branch(chunks[1], "bank5")
+        gate_branch(chunks[4], "bank2")
+        linear_branch(chunks[2], "bank6")
+        gate_branch(chunks[5], "bank3")
+        linear_branch(chunks[3], "bank7")
+        hidden(chunks[0])
+        gate_branch(chunks[6], "bank4")
+        hidden(chunks[1])
+        gate_branch(chunks[7], "bank5")
+        linear_branch(chunks[4], "bank0")
+        tags = (("bank6", "bank4"), ("bank0", "bank7"), ("bank6", "bank5"), ("bank0", "bank2"))
+        for n in range(3):
+            hidden(chunks[2 * n + 2])
+            quantise_hidden(pairs[n], *tags[n])
+            if n == 0:
+                for late in range(1, 4):
+                    linear_branch(chunks[4 + late], f"bank{late}")
+            hidden(chunks[2 * n + 3])
+            put_lower(pairs[n])
+        quantise_hidden(pairs[3], *tags[3])
+        put_upper(0, CUT)
+        put_lower(pairs[3])
+        put_upper(CUT, S)
+        nc.sync.dma_start(out[P : 2 * P, :], windows[1][:])
+        nc.sync.dma_start(out[0:P, 0 : U // 2], windows[0][:, 0 : U // 2])
+        nc.scalar.dma_start(out[0:P, U // 2 : U], windows[0][:, U // 2 : U])

@@ -22,7 +22,7 @@ PACK = 4
 CHUNK = 128
 PAIR = 2 * CHUNK
 GATHER = 512
-CUT = 448
+CUT = 384
 
 
 def tile_picked_route2_glusilu_p_kernel(tc, x_words, x_scales, gate, w1, w3, w2_words, w2_scales, offs, dst, out):
@@ -52,8 +52,8 @@ def tile_picked_route2_glusilu_p_kernel(tc, x_words, x_scales, gate, w1, w3, w2_
         xw = reuse.tile([P, T], U32, name="xw", offset=9 * T // 2, align_bytes=64)
         nc.sync.dma_start(xw[:].bitcast(I32), x_words[0].rearrange("p n t -> p (n t)").bitcast(I32))
         w3_rows = w3.rearrange("(p j) c -> p j c", j=PACK)
-        w3_upper = reuse.tile([P, 2, H], F32, name="w3_upper", offset=7 * T // 2, align_bytes=64)
-        nc.sync.dma_start(w3_upper[:], w3_rows[:, 0:2, :])
+        w3_left = reuse.tile([P, PACK, H // 2], F32, name="w3_left", offset=7 * T // 2, align_bytes=64)
+        nc.sync.dma_start(w3_left[:], w3_rows[:, :, 0 : H // 2])
 
         def clear(window):
             nc.scalar.activation(
@@ -63,9 +63,9 @@ def tile_picked_route2_glusilu_p_kernel(tc, x_words, x_scales, gate, w1, w3, w2_
         clear(window1)
         nc.vector.memset(x_planes[:].bitcast(I32), 0)
 
-        def dealt(raw, grouped, t0, t1, j0, j1):
+        def dealt(raw, grouped, t0, t1, m0, m1):
             src = raw[:].rearrange("p j (m t) -> p m t j", t=PACK)[:, :, t0:t1, :]
-            to = grouped[:].rearrange("p (t m j) -> p m t j", m=P, j=PACK)[:, :, :, j0:j1]
+            to = grouped[:].rearrange("p (t m j) -> p m t j", m=P, j=PACK)[:, m0:m1]
             return to, src
 
         w1_bf = keep.tile([P, PACK * H], BF16, name="w1_bf", tag="w1_bf", align_bytes=64)
@@ -74,7 +74,7 @@ def tile_picked_route2_glusilu_p_kernel(tc, x_words, x_scales, gate, w1, w3, w2_
         w3_codes = keep.tile([P, H], U32, name="w3_codes", align_bytes=64)
         w3_scales = keep.tile([P, H], U8, name="w3_scales", align_bytes=64)
 
-        nc.scalar.copy(*dealt(w1_raw, w1_bf, 0, PACK, 0, PACK))
+        nc.scalar.copy(*dealt(w1_raw, w1_bf, 0, PACK, 0, P))
 
         picked_w = [keep.tile([P, GATHER], U32, name=f"picked_w{g}", align_bytes=64) for g in range(S // GATHER)]
         picked_s = keep.tile([P, S], U8, name="picked_s", align_bytes=64)
@@ -84,8 +84,8 @@ def tile_picked_route2_glusilu_p_kernel(tc, x_words, x_scales, gate, w1, w3, w2_
                 x_planes[r:P:32, :].bitcast(I32), picked_s[32 + 4 * r : 96 : 16, :].bitcast(I32)
             )
         w2w_at = 2 * T + 64
-        w3_lower = reuse.tile([P, 2, H], F32, name="w3_lower", offset=w2w_at + 2 * N, align_bytes=64)
-        nc.sync.dma_start(w3_lower[:], w3_rows[:, 2:4, :])
+        w3_right = reuse.tile([P, PACK, H // 2], F32, name="w3_right", offset=w2w_at + 2 * N, align_bytes=64)
+        nc.sync.dma_start(w3_right[:], w3_rows[:, :, H // 2 : H])
         window0 = reuse.tile([P, U], F32, name="window0", offset=9 * T, align_bytes=64)
         clear(window0)
         windows = [window0, window1]
@@ -174,9 +174,9 @@ def tile_picked_route2_glusilu_p_kernel(tc, x_words, x_scales, gate, w1, w3, w2_
         def put_upper(j0, j1):
             nc.vector.tensor_tensor(places(0, j0, j1), y_upper[:, j0:j1], gate_row[:, j0:j1], MULT)
 
-        for v, (raw, engine_copy) in enumerate(((w3_upper, nc.scalar.copy), (w3_lower, nc.vector.tensor_copy))):
+        for v, (raw, engine_copy) in enumerate(((w3_left, nc.scalar.copy), (w3_right, nc.vector.tensor_copy))):
             for u in range(2):
-                engine_copy(*dealt(raw, w3_bf[u], 2 * u, 2 * u + 2, 2 * v, 2 * v + 2))
+                engine_copy(*dealt(raw, w3_bf[u], 2 * u, 2 * u + 2, v * P // 2, (v + 1) * P // 2))
         for t0, t1 in ((0, 2), (2, 3), (3, 4)):
             cols = slice(t0 * P, t1 * P)
             u, at = divmod(t0, 2)

from contextlib import ExitStack

import concourse.mybir as mybir

K, T, S, H, N, U = 512, 4096, 1024, 512, 256, 2048
FLOPS = 2 * S * K * H * 2 + 2 * S * H * N

F32 = mybir.dt.float32
BF16 = mybir.dt.bfloat16
I32 = mybir.dt.int32
U32 = mybir.dt.uint32
U16 = mybir.dt.uint16
U8 = mybir.dt.uint8
FP8X4 = mybir.dt.float8_e4m3fn_x4
FP4X4 = mybir.dt.float4_e2m1fn_x4
MULT = mybir.AluOpType.mult
SILU = mybir.ActivationFunctionType.Silu
COPY = mybir.ActivationFunctionType.Copy

P = 128
PACK = 4
CHUNK = 128
PAIR = 2 * CHUNK
GATHER = 512
CUT = 384


def tile_picked_route2_glusilu_p_kernel(tc, x_words, x_scales, gate, w1, w3, w2_words, w2_scales, offs, dst, out):
    nc = tc.nc
    with ExitStack() as ctx:
        keep = ctx.enter_context(tc.tile_pool(name="keep", bufs=1))
        reuse = ctx.enter_context(tc.tile_pool(name="reuse", bufs=1))
        psum = ctx.enter_context(tc.psum_pool(name="psum", bufs=1))

        offs_sb = keep.tile([P, S // 16], U16, name="offs_sb")
        dst_sb = keep.tile([P, S // 16], U16, name="dst_sb")
        xs = reuse.tile([P, T], U8, name="xs", offset=2 * T, align_bytes=64)
        w1_raw = reuse.tile([P, PACK, H], F32, name="w1_raw", offset=9 * T, align_bytes=64)
        seed = reuse.tile([P, 32], F32, name="seed", offset=9 * T // 2 - 64, align_bytes=64)
        zeros = keep.tile([P, 32], F32, name="zeros")
        x_planes = keep.tile([P, S], U8, name="x_planes", align_bytes=64)
        window1 = keep.tile([P, U], F32, name="window1")

        w1_rows = w1.rearrange("(p j) c -> p j c", j=PACK)
        nc.sync.dma_start(w1_raw[:], w1_rows)
        nc.sync.dma_start(offs_sb[:], offs)
        nc.sync.dma_start(dst_sb[:], dst)
        nc.vector.memset(seed[:], 0.0)
        nc.vector.memset(xs[:].bitcast(I32), 0)
        nc.vector.tensor_copy(zeros[:], seed[:])
        nc.sync.dma_start(xs[32:96:4, :].bitcast(I32), x_scales[0].bitcast(I32))
        xw = reuse.tile([P, T], U32, name="xw", offset=9 * T // 2, align_bytes=64)
        nc.sync.dma_start(xw[:].bitcast(I32), x_words[0].rearrange("p n t -> p (n t)").bitcast(I32))
        w3_rows = w3.rearrange("(p j) c -> p j c", j=PACK)
        w3_left = reuse.tile([P, PACK, H // 2], F32, name="w3_left", offset=7 * T // 2, align_bytes=64)
        nc.sync.dma_start(w3_left[:], w3_rows[:, :, 0 : H // 2])

        def clear(window):
            nc.scalar.activation(
                window[:].rearrange("p (r c) -> p r c", c=32), zeros[:].unsqueeze(1).to_broadcast([P, U // 32, 32]), SILU
            )

        clear(window1)
        nc.vector.memset(x_planes[:].bitcast(I32), 0)

        def dealt(raw, grouped, t0, t1, m0, m1):
            src = raw[:].rearrange("p j (m t) -> p m t j", t=PACK)[:, :, t0:t1, :]
            to = grouped[:].rearrange("p (t m j) -> p m t j", m=P, j=PACK)[:, m0:m1]
            return to, src

        w1_bf = keep.tile([P, PACK * H], BF16, name="w1_bf", tag="w1_bf", align_bytes=64)
        w1_codes = keep.tile([P, H], U32, name="w1_codes", align_bytes=64)
        w3_bf = [keep.tile([P, PACK * H // 2], BF16, name=f"w3_bf{u}", tag=f"w3_bf{u}", align_bytes=64) for u in range(2)]
        w3_codes = keep.tile([P, H], U32, name="w3_codes", align_bytes=64)
        w3_scales = keep.tile([P, H], U8, name="w3_scales", align_bytes=64)

        nc.scalar.copy(*dealt(w1_raw, w1_bf, 0, PACK, 0, P))

        picked_w = [keep.tile([P, GATHER], U32, name=f"picked_w{g}", align_bytes=64) for g in range(S // GATHER)]
        picked_s = keep.tile([P, S], U8, name="picked_s", align_bytes=64)
        nc.vector.tensor_copy(picked_s[:], xs[:].indirect(offs_sb[:]))
        for r in range(4):
            nc.sync.dma_start(
                x_planes[r:P:32, :].bitcast(I32), picked_s[32 + 4 * r : 96 : 16, :].bitcast(I32)
            )
        w2w_at = 2 * T + 64
        w3_right = reuse.tile([P, PACK, H // 2], F32, name="w3_right", offset=w2w_at + 2 * N, align_bytes=64)
        nc.sync.dma_start(w3_right[:], w3_rows[:, :, H // 2 : H])
        window0 = reuse.tile([P, U], F32, name="window0", offset=9 * T, align_bytes=64)
        clear(window0)
        windows = [window0, window1]
        w2w = reuse.tile([P, 2 * N], U8, name="w2w", offset=w2w_at, align_bytes=64)
        nc.sync.dma_start(w2w[:].bitcast(I32), w2_words[0].bitcast(I32))
        gate_row = reuse.tile([P, S], F32, name="gate_row", offset=w2w_at - 4 * S, align_bytes=64)
        nc.sync.dma_start(gate_row[:], gate)
        w1_scales = keep.tile([P, H], U8, name="w1_scales", align_bytes=64)
        nc.vector.quantize_mx(out=w1_codes[:].bitcast(FP8X4), scales=w1_scales[:], in_=w1_bf[:])
        w2s = keep.tile([P, N], U8, name="w2s", align_bytes=64)
        nc.vector.memset(w2s[:].bitcast(I32), 0)
        for r in range(4):
            nc.gpsimd.dma_start(w2s[r:P:32, :].bitcast(I32), w2_scales[0, r:16:4, :].bitcast(I32))
        for g in range(S // GATHER):
            cols = slice(g * GATHER // 16, (g + 1) * GATHER // 16)
            nc.vector.tensor_copy(picked_w[g][:], xw[:].indirect(offs_sb[:, cols]))

        def first_product(bank, codes, scales, j0, j1):
            g, at = divmod(j0, GATHER)
            for t in range(PACK):
                nc.tensor.matmul_mx(
                    out=bank[:, t, :],
                    lhsT=codes[:, t * P : (t + 1) * P].bitcast(FP8X4),
                    lhsT_scale=scales[:, t * P : (t + 1) * P],
                    rhs=picked_w[g][:, at : at + j1 - j0].bitcast(FP8X4),
                    rhs_scale=x_planes[:, j0:j1],
                    start=True,
                    stop=True,
                )

        h_bf = keep.tile([P, S * PACK], BF16, name="h_bf", align_bytes=64)
        h_codes = keep.tile([P, S], U32, name="h_codes", align_bytes=64)
        h_scales = keep.tile([P, S], U8, name="h_scales", align_bytes=64)
        act = [keep.tile([P, CHUNK, PACK], F32, name=f"act{c}", align_bytes=64) for c in range(S // CHUNK)]
        linear = {}

        def gate_branch(c, tag):
            bank = psum.tile([P, PACK, CHUNK], F32, name=f"gate_bank{c}", tag=tag)
            first_product(bank, w1_codes, w1_scales, c * CHUNK, (c + 1) * CHUNK)
            nc.scalar.activation(act[c][:], bank[:].rearrange("p t n -> p n t"), SILU)

        def linear_branch(c, tag):
            bank = psum.tile([P, PACK, CHUNK], F32, name=f"linear_bank{c}", tag=tag)
            first_product(bank, w3_codes, w3_scales, c * CHUNK, (c + 1) * CHUNK)
            linear[c] = bank

        def hidden(c):
            to = h_bf[:, c * CHUNK * PACK : (c + 1) * CHUNK * PACK].rearrange("p (n t) -> p n t", t=PACK)
            nc.vector.tensor_tensor(to, linear[c][:].rearrange("p t n -> p n t"), act[c][:], MULT)

        def second_product(q, m, tag):
            bank = psum.tile([P, PAIR], F32, name=f"y_bank{m}_{q}", tag=tag)
            cols = slice(q * PAIR, (q + 1) * PAIR)
            nc.tensor.matmul_mx(
                out=bank[:],
                lhsT=w2w[:, 2 * m * P : 2 * (m + 1) * P].bitcast(FP4X4),
                lhsT_scale=w2s[:, m * P : (m + 1) * P],
                rhs=h_codes[:, cols].bitcast(FP8X4),
                rhs_scale=h_scales[:, cols],
                start=True,
                stop=True,
            )
            return bank

        y_upper = keep.tile([P, S], F32, name="y_upper")
        lower_banks = {}

        def quantise_hidden(q, lower_tag, upper_tag):
            cols = slice(q * PAIR, (q + 1) * PAIR)
            nc.vector.quantize_mx(
                out=h_codes[:, cols].bitcast(FP8X4),
                scales=h_scales[:, cols],
                in_=h_bf[:, q * PAIR * PACK : (q + 1) * PAIR * PACK],
            )
            lower_banks[q] = second_product(q, 1, lower_tag)
            nc.scalar.copy(y_upper[:, cols], second_product(q, 0, upper_tag)[:])

        def places(m, j0, j1):
            return windows[m][:].indirect(dst_sb[:, j0 // 16 : j1 // 16])

        def put_lower(q):
            weighed = keep.tile([P, PAIR], F32, name=f"weighed{q}")
            nc.vector.tensor_tensor(weighed[:], lower_banks[q][:], gate_row[:, q * PAIR : (q + 1) * PAIR], MULT)
            nc.scalar.activation(places(1, q * PAIR, (q + 1) * PAIR), weighed[:], COPY)

        def put_upper(j0, j1):
            nc.vector.tensor_tensor(places(0, j0, j1), y_upper[:, j0:j1], gate_row[:, j0:j1], MULT)

        for v, (raw, engine_copy) in enumerate(((w3_left, nc.scalar.copy), (w3_right, nc.vector.tensor_copy))):
            for u in range(2):
                engine_copy(*dealt(raw, w3_bf[u], 2 * u, 2 * u + 2, v * P // 2, (v + 1) * P // 2))
        for t0, t1 in ((0, 2), (2, 3), (3, 4)):
            cols = slice(t0 * P, t1 * P)
            u, at = divmod(t0, 2)
            nc.vector.quantize_mx(
                out=w3_codes[:, cols].bitcast(FP8X4),
                scales=w3_scales[:, cols],
                in_=w3_bf[u][:, at * P * PACK : (at + t1 - t0) * P * PACK],
            )
        pairs = (0, 1, 2, 3)
        chunks = [2 * q + e for q in pairs for e in range(2)]
        for n in range(4):
            gate_branch(chunks[n], f"bank{n}")
        linear_branch(chunks[0], "bank4")
        linear_branch(chunks[1], "bank5")
        gate_branch(chunks[4], "bank2")
        linear_branch(chunks[2], "bank6")
        gate_branch(chunks[5], "bank3")
        linear_branch(chunks[3], "bank7")
        hidden(chunks[0])
        gate_branch(chunks[6], "bank4")
        hidden(chunks[1])
        gate_branch(chunks[7], "bank5")
        linear_branch(chunks[4], "bank0")
        tags = (("bank6", "bank4"), ("bank0", "bank7"), ("bank6", "bank5"), ("bank0", "bank2"))
        for n in range(3):
            hidden(chunks[2 * n + 2])
            quantise_hidden(pairs[n], *tags[n])
            if n == 0:
                for late in range(1, 4):
                    linear_branch(chunks[4 + late], f"bank{late}")
            hidden(chunks[2 * n + 3])
            put_lower(pairs[n])
        quantise_hidden(pairs[3], *tags[3])
        put_upper(0, CUT)
        put_lower(pairs[3])
        put_upper(CUT, S)
        nc.sync.dma_start(out[P : 2 * P, :], windows[1][:])
        nc.sync.dma_start(out[0:P, 0 : U // 2], windows[0][:, 0 : U // 2])
        nc.scalar.dma_start(out[0:P, U // 2 : U], windows[0][:, U // 2 : U])
